import numpy as np, ml_dtypes
CORES = [211,219,227,235,243,251,83,91,99,107,115,123]
N = 12
TOK, K = 256, 3
ROUTE = [[[0,6,9],[2,3,10],[6,7,8],[1,2,7],[0,3,9],[0,2,11],[4,5,6],[4,6,11],[0,5,10],[0,3,6],[2,6,11],[5,7,9],[5,6,11],[0,2,10],[2,6,10],[1,3,5],[7,9,11],[0,2,5],[0,4,6],[5,7,10],[4,7,9],[2,6,8],[0,7,11],[3,9,10],[0,4,11],[5,7,9],[6,9,11],[4,5,9],[5,6,7],[2,5,11],[2,3,9],[7,9,10],[4,6,10],[8,10,11],[0,1,11],[3,4,8],[0,1,3],[1,2,7],[5,10,11],[4,5,7],[2,8,11],[2,4,5],[1,5,6],[3,5,6],[3,7,8],[4,7,11],[0,1,11],[0,3,9],[4,5,8],[2,5,6],[6,7,10],[0,3,6],[0,2,5],[3,8,9],[4,9,11],[2,9,11],[2,6,8],[1,2,4],[0,3,7],[2,3,6],[0,3,6],[0,6,8],[5,6,9],[3,6,8],[4,5,10],[1,5,6],[3,5,6],[1,4,7],[3,4,10],[6,9,10],[0,5,10],[0,3,9],[6,8,10],[2,4,6],[1,9,11],[3,6,11],[4,8,10],[1,6,11],[0,4,6],[5,6,10],[0,10,11],[1,6,10],[1,7,8],[0,7,9],[1,3,10],[0,7,11],[0,2,5],[7,9,10],[3,5,6],[2,4,7],[3,10,11],[2,4,8],[5,6,8],[7,10,11],[1,4,5],[3,5,10],[2,3,7],[7,10,11],[4,5,8],[4,6,9],[0,9,10],[4,7,10],[0,5,9],[1,3,9],[0,5,8],[1,7,10],[1,2,10],[0,4,6],[4,7,10],[4,7,9],[0,4,5],[1,3,11],[0,3,9],[4,5,11],[0,2,9],[2,3,11],[2,6,7],[5,9,10],[1,4,9],[1,7,8],[2,6,8],[1,3,7],[0,2,6],[0,6,7],[0,6,11],[1,2,5],[2,8,10],[0,5,9],[4,5,8],[2,5,10],[2,10,11],[9,10,11],[5,6,10],[0,2,11],[0,2,11],[3,5,7],[4,7,8],[0,2,6],[1,3,11],[2,9,11],[2,9,10],[2,5,9],[3,4,11],[1,3,4],[1,2,7],[6,7,10],[4,8,9],[5,7,10],[0,2,6],[2,3,8],[3,5,8],[5,7,10],[0,2,6],[8,10,11],[3,5,6],[3,9,10],[1,3,7],[0,2,11],[1,2,9],[7,8,9],[4,5,10],[0,3,4],[0,4,10],[0,2,4],[2,9,11],[1,2,9],[0,6,9],[7,9,11],[3,7,11],[1,4,5],[4,5,7],[0,2,11],[1,8,10],[1,3,9],[5,7,9],[2,5,7],[0,1,8],[2,5,10],[1,2,11],[2,6,11],[1,5,10],[3,10,11],[0,5,7],[0,6,9],[2,3,11],[0,6,11],[0,4,8],[1,2,11],[5,7,11],[4,7,10],[0,10,11],[1,3,10],[2,5,6],[8,9,10],[2,7,9],[0,3,11],[2,7,11],[4,5,9],[1,6,11],[2,4,6],[1,4,8],[3,4,9],[1,7,11],[5,7,8],[6,9,10],[0,1,9],[3,6,7],[1,6,9],[1,3,10],[2,7,10],[0,1,9],[1,10,11],[6,8,9],[2,5,8],[1,6,8],[2,4,8],[1,5,8],[6,8,10],[0,6,10],[1,4,11],[5,6,9],[4,9,11],[0,9,11],[0,7,11],[1,8,10],[1,3,7],[0,2,10],[2,9,11],[3,5,6],[2,3,4],[0,3,11],[3,8,9],[4,7,11],[5,8,9],[0,7,9],[6,8,11],[2,8,11],[5,7,8],[1,2,10],[1,4,6],[1,3,11],[1,7,8],[4,8,10],[3,5,10],[6,10,11],[2,3,10],[0,3,7],[5,8,10],[3,5,7],[5,6,10],[3,8,9],[2,4,5],[6,7,8],[0,6,8],[0,6,8],[1,5,7]],[[0,2,4],[5,9,11],[0,3,9],[2,8,11],[2,8,11],[2,3,11],[0,3,4],[1,4,8],[4,9,10],[0,9,10],[7,8,11],[6,8,11],[2,4,7],[0,4,9],[0,2,5],[4,8,10],[0,8,11],[5,8,9],[4,6,9],[1,10,11],[1,8,9],[1,6,7],[1,6,11],[2,9,10],[5,7,11],[1,3,4],[1,6,7],[3,5,10],[0,3,6],[5,8,10],[4,6,11],[5,9,11],[5,7,10],[4,6,7],[2,5,9],[2,3,9],[0,1,9],[3,4,8],[6,8,11],[1,7,11],[3,9,11],[1,2,7],[0,9,10],[2,3,5],[3,9,11],[2,10,11],[2,5,6],[3,5,6],[3,9,11],[2,7,11],[9,10,11],[2,5,7],[2,5,10],[6,8,10],[0,4,8],[5,7,10],[3,4,9],[0,7,8],[4,8,11],[2,4,6],[0,1,6],[0,7,10],[3,4,6],[3,6,11],[0,2,5],[2,9,10],[7,8,10],[5,9,10],[1,2,7],[3,6,8],[1,8,9],[0,2,7],[1,3,5],[1,4,5],[1,5,7],[0,6,8],[1,4,11],[0,6,7],[2,6,10],[0,2,4],[1,2,9],[1,2,6],[1,6,8],[1,6,8],[0,1,8],[3,7,8],[2,4,8],[3,6,8],[2,7,9],[1,9,11],[7,8,10],[7,8,9],[0,10,11],[4,10,11],[2,9,11],[0,6,8],[3,5,8],[4,6,9],[7,8,9],[1,2,5],[3,6,11],[0,8,10],[2,4,6],[2,7,8],[3,4,11],[2,6,11],[0,2,8],[1,2,11],[0,3,8],[4,9,11],[0,4,8],[0,7,9],[3,5,10],[0,2,10],[2,4,10],[1,3,4],[0,5,9],[1,2,9],[1,3,7],[0,1,9],[2,4,11],[0,8,9],[0,4,6],[6,7,11],[1,2,10],[8,10,11],[3,4,10],[3,8,11],[0,2,4],[5,7,8],[0,1,2],[0,9,11],[3,9,11],[0,2,5],[4,5,10],[4,10,11],[0,6,7],[2,8,9],[1,3,5],[3,4,5],[5,9,10],[2,5,11],[3,4,7],[3,8,10],[0,3,6],[2,6,9],[1,2,7],[1,10,11],[1,9,11],[2,8,11],[4,8,11],[2,6,7],[8,10,11],[7,8,9],[0,3,8],[3,7,10],[3,5,9],[4,10,11],[2,7,10],[2,7,9],[0,4,5],[2,7,11],[3,4,10],[3,5,8],[1,3,8],[0,3,5],[2,6,8],[3,7,10],[0,1,9],[3,5,6],[2,8,11],[4,5,9],[0,2,6],[1,6,10],[2,3,5],[1,2,4],[3,5,10],[0,5,7],[3,6,7],[3,7,10],[4,7,10],[2,3,5],[0,2,10],[6,8,10],[1,4,5],[1,3,11],[0,5,8],[4,7,11],[1,2,7],[1,10,11],[0,7,9],[0,4,11],[1,3,5],[2,3,8],[2,5,11],[2,8,9],[0,1,8],[1,3,10],[9,10,11],[2,5,6],[1,5,11],[0,2,7],[4,7,10],[1,6,9],[0,3,10],[1,2,7],[1,9,10],[1,2,4],[2,9,11],[3,5,9],[0,1,6],[4,8,10],[1,5,6],[0,7,8],[2,4,8],[3,10,11],[5,6,10],[0,3,4],[1,9,11],[4,6,7],[0,2,9],[2,3,10],[4,10,11],[6,7,11],[2,3,4],[0,3,11],[2,6,9],[2,5,10],[5,6,10],[0,2,9],[0,6,11],[0,1,2],[7,10,11],[3,4,10],[4,7,8],[4,5,11],[1,7,9],[2,4,5],[1,6,9],[7,8,10],[0,1,3],[1,5,8],[5,7,11],[3,10,11],[3,6,9],[0,6,7],[3,7,8],[0,3,4],[0,3,5],[4,5,11],[0,2,11],[1,2,7],[5,8,9],[2,6,7],[5,7,9],[3,4,6]],[[8,9,10],[1,8,11],[0,2,8],[2,3,5],[0,3,6],[1,3,8],[5,10,11],[4,5,8],[2,8,10],[3,6,9],[1,3,10],[2,7,8],[0,1,11],[2,7,10],[3,5,10],[0,2,7],[1,5,11],[1,6,9],[3,10,11],[6,7,9],[5,6,9],[3,4,11],[3,6,11],[0,3,11],[0,6,8],[1,2,4],[1,3,9],[2,7,11],[6,10,11],[4,6,10],[2,7,11],[2,3,8],[1,6,11],[3,7,8],[0,2,10],[6,8,11],[2,4,7],[0,2,3],[3,5,11],[0,2,3],[5,7,11],[1,10,11],[4,7,10],[2,7,8],[1,5,9],[6,8,11],[5,6,7],[0,2,5],[1,6,10],[5,6,8],[2,6,8],[1,8,9],[1,6,7],[2,3,4],[2,7,9],[0,3,11],[8,9,10],[0,2,6],[3,6,9],[0,10,11],[4,7,10],[6,8,9],[2,8,9],[3,5,7],[2,10,11],[2,3,6],[0,6,8],[0,8,10],[0,8,10],[0,4,5],[5,8,9],[2,8,10],[0,7,10],[2,10,11],[2,4,5],[5,8,9],[8,9,10],[2,6,11],[2,3,8],[1,2,5],[1,9,10],[3,7,11],[4,6,8],[3,4,5],[0,8,10],[1,8,9],[3,4,6],[3,4,7],[4,10,11],[1,4,6],[6,9,11],[0,7,11],[8,10,11],[5,8,9],[5,7,10],[8,9,10],[0,1,2],[0,3,11],[1,6,11],[3,8,9],[1,4,10],[3,4,6],[1,8,11],[4,5,11],[3,5,10],[4,6,9],[4,5,9],[8,10,11],[3,5,9],[1,3,5],[1,8,10],[1,3,10],[0,5,6],[7,9,11],[1,3,5],[4,7,10],[0,3,5],[1,7,9],[5,7,11],[2,6,10],[3,4,7],[0,3,6],[2,4,10],[1,2,7],[2,4,8],[4,7,8],[3,8,10],[3,4,11],[0,1,6],[3,8,10],[0,2,11],[2,7,10],[1,6,8],[0,2,7],[1,3,10],[7,8,10],[1,6,7],[0,2,5],[1,4,6],[0,8,10],[0,3,9],[5,6,7],[1,2,3],[1,7,8],[3,6,10],[0,2,3],[4,7,10],[5,8,10],[4,8,10],[0,2,4],[1,3,10],[1,4,7],[1,3,5],[3,7,10],[2,8,9],[1,8,10],[3,4,10],[0,1,8],[2,5,7],[5,8,11],[5,8,11],[5,6,11],[2,4,7],[5,6,8],[1,7,10],[0,1,4],[0,2,3],[3,4,6],[1,3,10],[1,10,11],[1,6,11],[0,3,7],[1,3,9],[3,5,6],[0,1,11],[1,3,10],[1,4,7],[2,5,9],[4,5,10],[2,8,10],[0,4,5],[5,7,10],[1,8,11],[0,2,7],[1,6,9],[0,9,11],[2,4,8],[0,6,8],[7,9,11],[0,1,11],[2,3,11],[3,6,8],[0,6,7],[6,7,10],[4,8,11],[1,4,11],[1,2,8],[1,2,7],[3,10,11],[1,6,7],[1,9,10],[1,2,9],[3,4,6],[0,3,11],[0,1,10],[1,3,4],[1,7,8],[9,10,11],[3,5,8],[8,10,11],[1,5,9],[6,7,9],[2,6,7],[4,7,11],[1,6,8],[2,3,7],[4,10,11],[0,6,7],[3,9,10],[4,6,8],[5,9,11],[3,9,10],[3,8,9],[0,1,4],[0,1,4],[0,7,10],[5,7,8],[2,8,10],[6,9,11],[4,8,11],[0,10,11],[3,9,10],[0,3,5],[5,10,11],[5,9,10],[6,8,9],[1,3,7],[0,3,7],[0,2,4],[4,5,11],[0,4,11],[1,5,10],[4,5,9],[0,2,9],[4,6,9],[1,2,9],[5,6,7],[6,7,10],[5,6,10],[2,5,6],[0,9,10],[7,8,11],[0,1,9],[2,4,9],[1,8,9],[2,5,8]],[[6,8,10],[1,4,6],[1,2,8],[1,2,7],[3,4,7],[3,8,9],[1,6,8],[0,2,3],[0,4,9],[5,6,9],[2,3,10],[0,1,2],[3,9,11],[1,3,8],[4,5,11],[6,7,10],[1,6,11],[7,10,11],[3,9,11],[7,8,10],[4,5,11],[3,6,9],[3,5,6],[2,3,6],[1,2,6],[2,3,5],[2,4,5],[1,6,8],[1,9,10],[0,5,10],[4,7,8],[1,10,11],[0,6,8],[2,7,8],[0,1,2],[0,3,8],[2,5,7],[0,2,8],[1,3,7],[0,5,8],[0,2,6],[4,5,6],[5,6,11],[3,9,11],[7,8,9],[1,3,5],[3,9,11],[0,3,6],[4,5,6],[1,2,10],[5,8,10],[2,7,10],[4,9,11],[2,6,11],[0,5,6],[3,5,9],[1,2,8],[3,7,9],[1,4,8],[2,6,8],[6,8,11],[7,9,11],[5,7,11],[2,3,11],[5,7,10],[7,10,11],[0,2,9],[0,8,9],[0,1,4],[0,1,7],[4,6,9],[3,6,9],[3,9,11],[2,5,11],[0,5,8],[0,4,9],[0,3,9],[0,6,10],[0,1,8],[0,8,10],[1,8,9],[4,10,11],[1,6,10],[2,4,8],[5,6,10],[5,7,11],[2,5,10],[1,5,8],[1,5,9],[2,6,7],[1,6,10],[1,3,4],[2,4,11],[0,4,5],[1,5,10],[2,3,6],[3,8,11],[4,5,10],[3,6,9],[0,2,5],[0,2,4],[6,8,11],[3,10,11],[4,6,7],[5,9,11],[4,5,6],[0,4,7],[6,8,10],[6,7,11],[0,5,6],[3,5,7],[2,3,10],[0,1,11],[2,3,8],[4,8,10],[1,2,3],[5,6,9],[4,10,11],[3,4,9],[4,9,11],[2,9,10],[2,7,10],[1,5,6],[1,6,8],[2,8,10],[0,1,3],[1,5,6],[0,9,11],[5,8,11],[2,7,11],[1,9,11],[1,2,3],[2,4,5],[3,6,11],[0,4,5],[4,5,7],[0,2,7],[0,8,11],[7,8,10],[2,10,11],[1,5,11],[4,7,10],[1,2,7],[2,7,11],[2,7,8],[5,7,10],[2,5,11],[0,3,5],[5,6,11],[0,3,4],[0,1,2],[2,6,11],[5,6,9],[0,4,9],[2,8,9],[2,4,8],[1,4,11],[2,7,10],[1,2,5],[3,7,9],[4,6,9],[3,6,11],[3,7,8],[5,6,8],[0,3,5],[0,5,8],[6,9,11],[1,5,7],[4,9,11],[1,7,8],[0,3,10],[5,7,9],[1,5,8],[1,10,11],[6,8,10],[3,7,10],[0,1,11],[2,4,8],[8,9,10],[2,7,9],[0,1,2],[4,8,10],[2,5,7],[4,5,6],[5,6,9],[1,3,5],[4,6,9],[2,4,9],[4,7,9],[0,6,9],[7,8,9],[4,6,9],[5,7,10],[5,7,11],[2,8,11],[4,5,7],[5,8,11],[2,3,6],[0,5,10],[3,5,8],[2,4,10],[4,9,11],[4,5,10],[0,1,8],[1,2,4],[7,9,11],[2,5,6],[4,9,11],[5,6,7],[3,4,8],[0,3,7],[1,3,10],[0,3,11],[0,7,10],[0,1,8],[0,7,11],[5,9,10],[1,5,9],[3,6,10],[4,6,7],[1,5,9],[2,6,9],[4,9,11],[1,7,11],[2,6,10],[5,10,11],[3,7,10],[5,8,9],[2,5,10],[0,2,6],[2,5,10],[2,3,4],[3,7,9],[5,9,10],[3,7,11],[1,2,5],[2,6,11],[0,1,3],[4,5,9],[3,7,10],[2,8,10],[3,4,11],[1,6,10],[7,9,10],[2,4,5],[2,4,6],[1,6,8],[2,7,8],[0,4,11],[3,4,6],[8,10,11],[1,4,10],[0,2,10],[1,5,10],[3,8,10],[3,4,5]],[[0,6,11],[0,2,3],[6,8,9],[0,2,7],[4,6,10],[2,3,11],[1,2,5],[3,9,10],[0,3,10],[3,6,10],[2,6,9],[2,3,9],[1,2,10],[1,6,9],[4,6,7],[4,10,11],[2,8,11],[1,2,7],[6,9,11],[0,5,8],[0,9,10],[6,8,10],[2,4,6],[6,8,10],[3,5,8],[2,5,11],[0,1,6],[0,7,8],[6,9,11],[3,4,6],[3,5,6],[7,10,11],[0,2,9],[2,4,5],[5,9,11],[3,10,11],[0,4,10],[3,6,9],[0,2,11],[0,9,11],[3,5,7],[1,3,5],[5,7,10],[0,1,4],[2,10,11],[0,6,10],[2,4,11],[5,7,8],[0,3,11],[2,3,8],[1,2,3],[1,4,9],[6,10,11],[3,7,9],[4,5,9],[4,5,9],[4,7,10],[1,3,5],[1,2,8],[0,1,10],[2,6,10],[2,7,10],[3,6,9],[2,4,10],[0,2,11],[4,10,11],[0,5,6],[0,2,10],[4,10,11],[5,6,11],[3,4,9],[0,5,9],[4,7,10],[4,8,10],[0,8,11],[2,3,5],[0,10,11],[3,5,10],[1,7,10],[0,2,5],[5,6,10],[1,2,8],[3,4,7],[3,9,10],[4,9,11],[1,5,8],[1,4,11],[0,6,10],[6,10,11],[5,7,9],[1,4,5],[0,1,2],[0,6,8],[5,6,9],[2,5,10],[3,5,8],[3,7,10],[0,2,6],[0,4,9],[3,6,9],[2,6,8],[1,3,9],[0,7,8],[6,7,8],[1,4,8],[3,4,9],[2,3,6],[0,6,9],[7,8,11],[4,5,7],[1,8,11],[1,8,10],[1,2,5],[5,8,10],[0,5,11],[4,8,11],[9,10,11],[8,9,10],[2,3,8],[0,8,11],[0,1,2],[7,10,11],[1,3,11],[5,9,10],[2,5,8],[1,5,9],[5,9,11],[2,3,5],[1,6,11],[3,8,11],[2,3,6],[1,4,11],[0,8,11],[7,8,10],[0,3,9],[0,2,4],[4,7,8],[0,3,7],[1,7,10],[1,3,11],[2,3,10],[6,7,10],[0,4,5],[1,6,9],[4,5,11],[1,3,8],[5,10,11],[1,7,9],[8,9,11],[1,5,6],[2,7,8],[1,4,7],[0,6,9],[4,6,11],[8,9,10],[0,7,9],[1,3,6],[4,7,9],[0,9,10],[7,10,11],[0,3,9],[3,9,10],[4,5,6],[1,6,9],[2,4,9],[3,5,9],[6,7,9],[7,8,11],[2,4,8],[0,2,9],[0,3,11],[0,3,4],[0,10,11],[1,6,9],[4,10,11],[0,1,8],[2,3,9],[4,7,10],[3,10,11],[2,5,10],[2,3,7],[3,7,8],[0,3,7],[1,5,11],[1,3,7],[0,4,7],[6,7,9],[0,8,11],[3,5,10],[0,8,11],[0,4,6],[3,4,6],[3,6,7],[3,7,8],[0,8,9],[0,4,8],[2,3,4],[4,5,7],[1,3,4],[1,6,10],[1,2,6],[1,2,10],[1,4,5],[1,4,11],[5,7,10],[2,4,9],[3,5,6],[0,2,8],[5,6,9],[0,2,10],[1,2,6],[1,6,11],[2,6,8],[9,10,11],[0,10,11],[2,3,5],[5,6,9],[5,7,8],[0,2,3],[1,7,10],[2,7,10],[5,8,11],[0,6,7],[5,9,10],[5,7,9],[4,8,9],[2,8,11],[1,2,4],[2,7,9],[1,4,7],[5,6,8],[1,5,7],[0,3,10],[2,3,4],[1,5,6],[1,5,8],[0,1,9],[0,5,10],[0,2,6],[0,4,7],[1,4,7],[0,2,9],[2,6,11],[1,6,7],[6,8,11],[1,3,5],[2,7,8],[3,5,8],[5,6,8],[1,8,11],[1,4,5],[0,1,10],[1,3,4],[2,3,7],[6,7,8],[0,5,7]],[[2,9,11],[8,9,10],[0,5,9],[1,3,4],[1,5,8],[3,4,9],[1,4,6],[2,3,5],[0,1,10],[0,5,7],[3,4,8],[5,7,10],[2,3,10],[2,3,8],[4,9,11],[5,10,11],[3,4,8],[4,8,11],[3,4,6],[3,5,6],[3,7,11],[3,9,11],[0,3,11],[1,7,9],[1,7,10],[1,3,10],[0,2,6],[0,4,11],[0,3,5],[3,6,10],[3,4,9],[2,4,11],[1,2,9],[2,4,9],[4,6,8],[3,7,10],[0,8,9],[4,7,11],[0,2,8],[5,9,11],[8,9,10],[0,3,11],[6,7,11],[2,8,9],[2,6,7],[0,8,9],[3,4,6],[0,1,7],[5,7,10],[2,5,10],[2,9,10],[4,5,7],[1,3,8],[1,3,10],[5,7,8],[4,9,11],[1,6,8],[3,8,11],[7,8,10],[3,7,8],[2,4,8],[0,6,10],[6,7,9],[4,6,9],[8,10,11],[4,5,9],[1,7,8],[2,6,10],[5,6,7],[9,10,11],[7,8,10],[4,9,11],[3,4,10],[1,5,9],[0,6,11],[5,7,11],[2,3,5],[3,6,11],[3,9,11],[0,2,6],[1,2,8],[1,4,6],[4,8,9],[6,9,11],[1,2,4],[0,6,9],[2,9,11],[3,4,6],[2,4,9],[0,1,4],[0,7,11],[1,4,8],[0,3,5],[3,4,5],[2,7,10],[5,6,7],[7,8,11],[3,4,9],[2,6,11],[2,3,4],[1,2,11],[2,8,10],[2,4,11],[2,4,9],[8,9,11],[2,8,11],[0,6,9],[0,1,4],[6,9,11],[0,6,9],[2,3,9],[5,6,11],[1,3,11],[8,9,10],[0,2,5],[1,6,11],[2,6,8],[3,6,9],[1,7,9],[4,7,9],[4,6,8],[1,7,11],[4,6,11],[6,9,10],[0,1,10],[4,7,10],[2,7,10],[2,8,10],[0,6,10],[0,4,8],[4,9,11],[2,4,8],[9,10,11],[2,6,7],[3,6,8],[3,7,11],[0,8,9],[4,6,11],[3,4,8],[3,9,11],[0,1,9],[6,7,11],[2,7,9],[1,4,8],[1,6,10],[0,3,6],[1,3,8],[0,2,5],[0,9,11],[4,8,11],[1,2,8],[1,2,8],[2,7,10],[0,8,9],[6,10,11],[3,6,8],[9,10,11],[0,6,9],[6,7,8],[0,2,7],[5,10,11],[4,7,8],[3,6,7],[2,3,8],[1,4,6],[1,2,4],[0,5,11],[1,9,11],[4,5,8],[4,9,10],[0,9,10],[4,10,11],[3,7,9],[1,4,11],[6,8,10],[1,2,10],[2,5,11],[1,4,5],[0,3,5],[0,1,6],[0,1,4],[1,7,9],[5,9,11],[2,3,7],[3,5,10],[0,1,7],[2,5,10],[0,3,9],[3,4,10],[1,10,11],[7,10,11],[3,9,11],[5,6,10],[7,10,11],[5,9,10],[4,5,7],[0,6,9],[0,2,8],[7,10,11],[8,9,11],[0,2,11],[0,4,9],[2,6,8],[3,4,8],[5,6,7],[5,6,7],[0,4,7],[0,4,11],[0,5,6],[0,1,7],[6,7,11],[3,6,9],[5,8,11],[4,10,11],[6,7,9],[3,4,8],[2,5,8],[0,4,8],[6,7,10],[2,3,7],[2,9,10],[2,3,9],[5,7,11],[4,8,9],[0,1,5],[4,6,11],[1,8,10],[1,2,3],[0,5,10],[0,2,4],[4,5,6],[1,6,7],[3,4,5],[1,7,9],[5,6,7],[2,4,6],[2,8,9],[1,4,7],[3,8,10],[0,5,6],[2,5,9],[0,10,11],[6,10,11],[0,3,10],[1,3,11],[2,4,9],[2,4,6],[2,6,9],[0,4,7],[4,5,7],[1,4,10],[2,3,7],[1,4,7],[2,4,5],[3,6,11],[2,3,4]],[[6,7,8],[2,10,11],[0,3,5],[3,4,10],[5,8,9],[0,5,11],[4,6,9],[2,3,4],[2,5,7],[0,2,11],[1,6,9],[0,2,10],[0,1,11],[0,3,4],[7,8,9],[0,4,11],[2,4,11],[1,7,10],[4,8,10],[3,7,10],[1,2,8],[2,6,7],[2,8,11],[1,6,11],[1,3,9],[0,5,9],[0,1,3],[8,9,10],[3,7,8],[5,7,9],[0,6,7],[1,5,10],[1,4,7],[3,8,9],[1,4,10],[1,6,11],[0,9,10],[1,6,8],[4,5,8],[2,4,7],[3,5,8],[0,7,9],[3,6,9],[0,4,9],[5,9,10],[3,4,7],[4,5,6],[5,8,10],[0,6,7],[3,6,9],[3,4,9],[2,3,11],[1,9,10],[0,1,10],[1,6,11],[3,10,11],[8,9,11],[3,5,6],[0,6,9],[0,7,9],[2,9,11],[2,5,6],[2,9,11],[0,6,11],[1,6,10],[1,2,7],[4,10,11],[1,3,5],[1,6,9],[2,9,11],[3,5,11],[3,9,11],[2,4,5],[0,1,5],[3,6,10],[3,4,5],[5,6,9],[1,4,8],[1,2,9],[9,10,11],[4,10,11],[0,1,8],[3,6,10],[0,3,5],[0,1,8],[0,1,5],[1,6,9],[1,6,9],[4,6,8],[1,2,9],[0,1,5],[0,3,6],[4,6,7],[2,3,10],[6,8,9],[4,8,10],[0,5,11],[3,4,5],[6,10,11],[1,4,7],[1,3,5],[5,6,8],[1,5,10],[3,4,10],[3,5,10],[5,8,9],[3,5,8],[1,5,9],[3,8,9],[7,8,11],[0,9,11],[1,5,9],[0,1,8],[1,4,8],[3,5,10],[5,6,11],[3,4,9],[1,6,11],[0,2,7],[2,4,10],[2,3,10],[0,1,10],[2,7,9],[8,9,10],[1,6,7],[1,5,9],[6,7,9],[6,10,11],[0,2,4],[1,10,11],[0,4,8],[5,7,10],[5,7,9],[2,3,11],[5,7,8],[0,6,7],[0,4,10],[2,4,6],[0,1,11],[5,9,10],[0,1,10],[1,3,5],[1,7,10],[1,6,10],[0,5,10],[2,9,11],[0,9,10],[0,4,6],[2,5,10],[3,5,9],[4,9,11],[0,5,11],[2,5,9],[5,10,11],[2,4,11],[2,6,10],[0,3,8],[5,7,10],[0,4,8],[0,5,10],[1,2,8],[2,3,6],[0,8,11],[0,5,6],[1,2,10],[1,10,11],[0,1,8],[8,10,11],[0,8,9],[3,5,11],[6,7,11],[2,6,7],[2,4,9],[1,3,7],[0,9,10],[2,8,11],[1,2,9],[0,1,4],[2,6,7],[1,6,10],[1,2,3],[0,10,11],[0,6,8],[3,10,11],[7,8,10],[0,3,10],[3,8,9],[2,10,11],[1,6,11],[4,6,9],[5,6,9],[2,3,4],[3,4,11],[6,7,8],[4,5,6],[4,6,10],[1,7,11],[6,8,11],[0,2,7],[0,3,8],[0,2,7],[4,6,10],[0,1,11],[0,1,5],[3,5,10],[0,4,6],[1,4,5],[1,2,6],[0,2,8],[1,4,6],[0,2,9],[0,2,3],[0,3,7],[2,3,5],[0,4,8],[0,3,4],[7,9,10],[2,3,9],[4,7,9],[5,6,11],[3,9,11],[3,7,10],[4,6,7],[1,2,6],[1,4,6],[0,7,11],[1,4,6],[1,6,8],[5,6,8],[1,4,5],[2,4,11],[2,4,9],[2,4,9],[2,3,5],[2,10,11],[0,4,7],[3,4,7],[2,6,7],[8,9,11],[1,4,10],[6,7,8],[0,4,10],[0,1,9],[3,8,10],[1,8,9],[6,7,8],[1,8,9],[2,9,10],[0,6,8],[4,9,10],[3,5,9],[2,7,9],[0,5,11],[1,8,10],[0,4,6],[7,10,11]],[[1,2,11],[4,5,7],[1,9,11],[2,7,10],[7,10,11],[0,2,3],[1,2,10],[0,2,3],[3,6,8],[1,8,11],[5,7,9],[0,3,6],[3,10,11],[4,6,7],[0,2,10],[1,2,3],[0,3,6],[2,3,4],[1,7,8],[2,8,9],[1,3,6],[6,7,10],[5,9,10],[1,4,11],[2,3,5],[0,2,3],[1,2,9],[0,7,8],[0,4,7],[1,4,10],[1,7,10],[1,7,9],[0,3,8],[0,3,11],[0,2,7],[3,7,10],[6,7,11],[8,10,11],[3,4,10],[0,2,4],[5,9,11],[1,4,5],[1,5,9],[6,7,10],[1,6,8],[4,8,9],[3,10,11],[7,8,10],[4,10,11],[1,3,11],[2,3,10],[0,6,11],[4,5,8],[1,8,9],[4,8,9],[0,3,11],[2,4,11],[0,2,3],[2,4,8],[4,5,6],[4,8,9],[5,8,9],[1,3,9],[0,8,11],[0,6,7],[0,3,9],[1,6,9],[2,9,10],[0,5,9],[5,8,11],[0,4,11],[1,5,6],[2,3,8],[4,6,11],[2,5,7],[0,9,10],[0,4,8],[5,7,8],[4,5,10],[2,8,9],[1,3,8],[2,9,11],[0,2,10],[3,9,10],[6,10,11],[1,6,11],[0,3,10],[1,10,11],[1,2,7],[3,8,9],[2,6,7],[1,6,10],[6,8,9],[0,2,5],[1,9,10],[1,4,5],[2,7,9],[1,5,8],[4,8,11],[0,9,10],[5,6,9],[0,8,11],[4,5,7],[4,8,10],[2,4,7],[2,4,11],[0,8,11],[4,9,11],[2,7,10],[0,3,11],[2,8,10],[2,5,11],[3,4,5],[3,4,9],[1,10,11],[2,4,7],[1,5,11],[2,6,7],[6,7,11],[4,7,10],[1,5,7],[3,5,11],[1,5,9],[1,7,9],[3,6,7],[4,8,11],[3,5,10],[1,2,3],[3,6,11],[0,7,10],[2,7,11],[0,1,5],[6,10,11],[2,7,11],[1,5,8],[7,8,10],[0,6,9],[2,5,10],[0,8,11],[0,7,8],[3,8,11],[2,3,10],[0,3,7],[0,6,11],[1,7,8],[3,4,5],[3,4,10],[5,6,11],[3,4,10],[0,7,8],[1,5,6],[1,3,9],[5,6,8],[5,6,10],[3,5,6],[1,2,6],[3,7,11],[0,3,4],[4,6,7],[1,2,3],[0,1,9],[2,6,8],[6,10,11],[1,8,10],[8,9,10],[0,1,3],[2,8,11],[1,6,10],[4,8,11],[3,8,10],[0,4,6],[1,5,7],[2,3,6],[6,7,11],[4,5,9],[1,3,11],[6,10,11],[3,4,7],[0,1,11],[3,9,10],[0,1,11],[0,3,5],[0,2,6],[1,4,6],[7,8,9],[4,10,11],[1,3,8],[3,5,10],[0,8,9],[0,2,4],[2,5,8],[0,2,9],[1,3,4],[7,8,10],[1,2,3],[2,3,11],[2,5,8],[0,9,10],[1,3,8],[6,7,8],[2,4,5],[2,4,5],[0,1,11],[4,5,6],[1,2,8],[1,2,7],[6,7,8],[4,8,10],[0,5,8],[1,4,11],[3,8,9],[1,7,9],[1,5,9],[5,6,10],[7,9,10],[3,9,11],[1,5,9],[0,1,4],[2,3,10],[0,2,8],[1,8,9],[6,7,11],[1,5,7],[1,4,6],[6,7,11],[0,4,8],[2,5,10],[1,4,11],[7,9,10],[0,10,11],[1,4,8],[1,8,9],[5,6,10],[4,10,11],[6,7,8],[5,7,8],[0,1,2],[0,8,9],[0,2,10],[3,7,10],[4,7,11],[1,2,6],[0,5,8],[4,5,11],[3,4,6],[3,7,10],[0,1,6],[3,4,8],[5,8,9],[3,4,9],[2,3,8],[3,8,11],[4,7,8],[0,3,11],[5,7,9],[3,5,6]],[[3,7,10],[1,2,6],[2,5,10],[0,3,6],[0,2,9],[5,7,9],[1,8,10],[2,7,9],[0,4,8],[1,5,9],[4,9,11],[3,5,7],[1,4,10],[1,6,7],[3,4,6],[3,7,8],[0,9,10],[4,7,8],[2,3,11],[4,5,7],[0,9,11],[1,5,11],[0,2,11],[6,8,11],[3,4,5],[1,8,9],[3,8,11],[2,5,7],[0,5,7],[2,7,11],[4,7,11],[2,5,10],[3,6,11],[6,9,10],[3,6,9],[9,10,11],[2,7,11],[1,5,8],[1,5,7],[0,6,7],[6,10,11],[6,7,11],[4,5,6],[3,10,11],[0,4,10],[0,7,11],[2,5,11],[4,6,8],[6,10,11],[3,7,10],[3,8,11],[3,10,11],[4,5,10],[2,3,8],[1,2,6],[4,7,8],[1,2,9],[2,4,10],[5,7,8],[2,6,10],[3,10,11],[0,2,9],[2,7,11],[2,10,11],[5,9,10],[5,9,10],[3,7,8],[0,4,7],[0,1,3],[3,6,7],[3,4,5],[2,4,6],[5,7,10],[1,4,10],[0,1,6],[5,10,11],[1,2,6],[1,8,11],[1,4,9],[0,1,9],[1,7,9],[2,8,9],[3,6,10],[2,3,11],[3,9,10],[0,6,7],[1,2,11],[1,4,7],[0,1,7],[3,6,11],[6,9,10],[0,3,11],[1,4,5],[3,5,10],[4,6,10],[7,10,11],[3,5,11],[4,7,10],[0,4,9],[3,5,11],[1,2,4],[1,6,11],[2,3,11],[4,7,9],[1,6,7],[9,10,11],[4,5,11],[0,3,8],[3,6,7],[2,9,11],[2,4,10],[2,8,11],[3,4,9],[0,1,8],[2,3,5],[3,8,9],[0,1,7],[2,7,11],[1,2,7],[1,6,7],[3,5,7],[1,6,7],[2,6,11],[1,4,5],[1,2,6],[0,8,9],[2,5,10],[1,2,5],[0,4,11],[7,10,11],[0,4,6],[1,4,9],[0,1,9],[1,4,10],[1,8,10],[2,6,7],[1,9,10],[5,6,9],[4,6,10],[0,5,7],[2,7,11],[2,8,11],[1,9,10],[8,9,11],[0,2,9],[5,10,11],[1,5,8],[1,3,6],[0,2,11],[3,7,9],[2,6,11],[0,1,10],[0,5,7],[0,4,11],[4,5,11],[0,1,7],[2,3,8],[2,3,8],[4,5,9],[5,6,7],[2,7,9],[6,7,9],[3,7,9],[0,3,8],[8,10,11],[1,9,10],[0,2,6],[1,5,6],[0,2,3],[0,1,4],[0,1,10],[6,7,10],[3,5,11],[1,6,7],[1,8,10],[2,7,8],[0,1,7],[2,4,11],[3,7,9],[6,7,10],[2,4,6],[3,7,9],[3,10,11],[2,3,6],[2,4,8],[3,6,9],[0,3,8],[4,5,9],[2,3,10],[2,8,9],[2,6,10],[3,6,8],[0,3,5],[4,7,11],[0,3,11],[2,3,9],[0,2,3],[4,7,9],[0,4,11],[4,6,10],[2,3,11],[5,7,9],[8,9,11],[0,1,6],[5,9,11],[1,2,7],[0,6,10],[0,1,10],[1,2,10],[5,6,11],[3,4,11],[8,9,10],[6,7,10],[0,1,8],[2,8,10],[0,3,7],[2,10,11],[0,3,11],[3,4,5],[4,6,11],[2,3,7],[5,9,11],[3,9,10],[1,2,6],[2,5,10],[6,9,11],[0,3,10],[2,7,11],[2,8,9],[1,6,8],[1,2,3],[0,3,5],[2,3,4],[0,4,5],[0,3,8],[4,9,11],[3,5,8],[3,5,8],[4,6,9],[0,6,7],[0,5,10],[0,5,6],[4,8,10],[2,4,10],[4,6,10],[0,1,2],[0,5,11],[0,2,3],[0,2,10],[4,8,11],[0,2,6],[1,5,6],[2,6,10],[6,7,11],[6,9,11],[1,7,8]],[[0,6,9],[4,8,11],[3,4,6],[7,8,10],[1,7,11],[2,7,8],[1,6,10],[1,3,5],[2,10,11],[0,1,4],[0,4,10],[2,8,11],[1,2,7],[0,1,11],[4,5,11],[1,4,9],[1,3,9],[0,1,10],[6,10,11],[4,5,9],[1,4,10],[3,6,11],[7,9,10],[5,6,9],[1,5,9],[2,7,11],[0,2,5],[3,5,10],[1,4,6],[0,6,8],[6,7,11],[1,7,8],[1,2,4],[3,5,11],[4,5,6],[0,1,4],[6,7,8],[3,10,11],[2,6,9],[1,2,3],[0,3,9],[2,7,10],[3,4,11],[3,5,10],[4,5,9],[3,9,11],[2,5,8],[1,8,9],[1,6,7],[0,1,3],[1,4,8],[3,7,10],[0,5,6],[1,4,7],[4,8,10],[2,8,9],[2,7,9],[4,7,9],[3,6,10],[4,5,8],[2,3,8],[6,8,9],[0,4,11],[1,5,9],[2,6,8],[6,7,10],[3,6,11],[0,3,4],[2,6,8],[8,9,11],[0,1,3],[2,3,11],[2,3,10],[0,6,10],[1,2,7],[1,4,5],[4,6,7],[8,10,11],[0,6,8],[6,8,9],[7,9,10],[0,2,4],[0,4,11],[4,8,9],[2,3,9],[2,8,11],[1,8,10],[0,1,8],[3,7,9],[3,9,10],[7,8,10],[7,10,11],[2,6,8],[0,10,11],[1,3,8],[3,10,11],[7,8,9],[4,5,11],[1,5,10],[3,4,11],[0,2,7],[0,1,4],[0,9,10],[0,4,11],[6,9,11],[1,3,6],[0,5,9],[0,4,10],[0,4,9],[4,6,9],[5,7,8],[2,5,10],[0,2,6],[5,7,8],[0,3,9],[1,3,8],[0,5,8],[2,6,11],[3,4,7],[3,5,8],[3,4,11],[1,3,10],[6,8,11],[1,3,6],[1,2,10],[5,8,10],[1,2,6],[3,4,8],[4,6,9],[6,10,11],[4,6,8],[4,5,8],[2,6,9],[0,5,8],[2,8,9],[0,1,10],[4,5,7],[2,8,11],[4,8,11],[2,3,7],[1,6,8],[1,7,9],[2,6,11],[0,5,11],[0,2,8],[0,1,6],[2,9,11],[1,2,4],[2,5,11],[2,9,11],[1,5,7],[0,3,9],[3,5,8],[4,5,11],[4,6,11],[0,3,11],[2,7,10],[3,7,11],[1,2,11],[7,9,11],[1,3,6],[7,8,11],[2,5,9],[2,3,10],[0,1,6],[0,10,11],[1,7,8],[3,6,10],[5,8,11],[5,6,8],[4,9,11],[2,10,11],[2,5,10],[5,7,11],[0,5,7],[1,3,10],[2,4,8],[3,7,9],[0,1,7],[1,5,6],[2,3,8],[0,3,8],[0,3,8],[5,9,10],[4,6,9],[3,10,11],[0,7,10],[2,4,7],[2,4,11],[3,4,11],[2,5,11],[0,8,11],[1,8,10],[1,2,9],[1,4,6],[3,6,11],[6,7,11],[0,8,11],[0,4,11],[7,9,11],[3,5,7],[6,8,10],[0,5,7],[0,6,11],[1,7,8],[8,10,11],[1,3,11],[4,7,9],[8,9,10],[0,2,11],[0,1,5],[1,3,7],[4,5,8],[1,5,10],[1,6,7],[3,4,6],[1,8,9],[2,5,7],[1,4,7],[3,7,11],[1,5,6],[6,7,8],[0,4,5],[9,10,11],[3,6,8],[0,1,2],[0,2,8],[0,1,11],[0,3,7],[3,4,7],[3,6,8],[7,8,9],[1,3,6],[0,4,11],[1,4,6],[6,8,9],[2,4,7],[3,6,7],[8,9,10],[2,5,6],[4,6,11],[5,9,11],[3,10,11],[8,9,11],[0,7,9],[2,3,5],[0,3,6],[3,4,6],[6,8,10],[2,10,11],[2,5,7],[1,3,5],[3,4,5],[1,2,7],[6,7,11],[4,5,10]],[[2,5,6],[0,4,5],[4,7,10],[2,3,8],[0,5,9],[5,7,9],[1,6,7],[3,5,9],[2,4,11],[5,10,11],[0,2,11],[6,9,11],[0,7,8],[7,10,11],[4,6,10],[0,5,10],[3,4,5],[3,6,7],[3,8,9],[2,7,8],[5,6,9],[3,7,8],[4,5,10],[1,4,10],[0,4,8],[0,4,8],[5,9,11],[0,9,10],[0,8,9],[2,3,7],[5,6,8],[0,1,8],[0,4,5],[5,7,8],[1,3,8],[0,3,5],[1,10,11],[1,7,9],[6,9,10],[7,8,11],[0,2,4],[3,4,10],[7,8,9],[0,2,10],[0,1,2],[1,6,11],[4,5,8],[2,3,5],[5,6,7],[3,4,6],[8,9,11],[4,5,10],[0,5,9],[6,7,8],[1,4,9],[5,8,10],[1,2,10],[0,3,11],[3,7,8],[3,4,9],[0,2,6],[1,4,10],[3,7,10],[0,1,3],[1,4,7],[6,7,8],[1,8,10],[1,3,7],[0,5,7],[4,5,6],[0,5,7],[0,7,9],[3,9,10],[4,7,9],[7,8,10],[5,7,11],[2,3,10],[2,7,11],[8,10,11],[7,10,11],[3,7,8],[1,5,9],[2,3,4],[5,6,10],[1,4,8],[2,7,8],[3,4,9],[1,6,10],[3,5,7],[1,7,11],[1,4,11],[0,1,5],[1,7,10],[3,5,10],[2,5,8],[5,7,9],[1,3,6],[2,3,6],[1,2,11],[0,1,8],[2,3,10],[1,4,8],[3,4,6],[1,4,5],[4,5,9],[4,10,11],[6,9,11],[1,2,5],[0,3,8],[0,2,5],[1,6,11],[1,3,7],[7,8,10],[3,4,6],[5,6,7],[3,7,9],[0,2,4],[0,5,7],[1,3,11],[1,5,9],[0,2,8],[0,7,11],[1,3,4],[1,4,5],[4,6,9],[3,6,8],[2,6,10],[0,8,11],[3,6,10],[3,9,10],[1,9,11],[2,5,10],[2,5,6],[2,5,6],[0,2,6],[0,4,9],[6,8,10],[7,8,9],[3,7,8],[0,3,5],[5,6,7],[0,9,10],[0,4,5],[2,6,8],[3,5,10],[3,5,9],[6,8,11],[3,8,10],[3,5,7],[3,6,7],[4,5,11],[0,3,11],[3,9,11],[3,9,10],[3,7,10],[0,1,11],[4,8,11],[1,3,4],[2,8,11],[2,5,7],[4,5,8],[4,8,11],[0,5,9],[0,3,7],[0,2,6],[0,4,5],[0,3,10],[0,2,10],[2,8,10],[1,3,5],[2,3,4],[6,8,10],[0,3,9],[5,9,10],[6,10,11],[3,8,11],[9,10,11],[5,7,11],[3,5,9],[0,3,8],[5,8,9],[4,6,10],[5,9,10],[4,6,11],[5,7,11],[2,3,8],[3,9,11],[4,6,8],[6,7,9],[2,9,10],[0,1,7],[3,5,8],[4,9,11],[1,3,11],[1,2,4],[3,4,9],[7,9,10],[2,3,5],[3,5,10],[4,9,11],[0,4,10],[0,4,6],[0,1,9],[2,3,10],[3,4,8],[0,5,6],[0,6,8],[2,9,11],[2,5,10],[1,4,8],[6,8,10],[1,4,10],[4,7,9],[3,5,11],[3,9,11],[0,1,9],[3,9,10],[4,6,11],[1,4,10],[0,5,10],[0,4,8],[1,7,8],[3,7,8],[6,7,11],[5,6,10],[1,4,7],[3,5,7],[0,1,3],[4,7,11],[0,3,11],[0,3,11],[3,9,10],[0,7,11],[7,8,10],[3,10,11],[7,8,9],[5,9,11],[2,4,6],[1,8,9],[4,5,6],[2,3,5],[0,2,8],[1,4,11],[0,3,10],[5,10,11],[2,4,7],[2,4,10],[0,5,11],[0,5,9],[2,6,11],[0,2,3],[6,9,11],[0,8,11],[0,3,10],[0,2,9],[1,6,8]],[[1,8,11],[1,8,11],[3,6,10],[0,1,8],[0,6,9],[3,4,9],[2,6,11],[1,3,8],[3,8,10],[6,8,9],[0,10,11],[6,7,8],[0,1,4],[2,6,7],[3,5,6],[1,3,9],[0,3,6],[1,5,7],[3,8,11],[2,5,9],[0,10,11],[4,9,11],[7,9,10],[3,5,9],[0,3,6],[1,8,10],[0,4,10],[8,9,10],[2,3,10],[6,8,10],[1,2,6],[0,5,8],[1,5,11],[6,9,11],[1,9,11],[3,7,10],[4,7,10],[2,4,9],[0,8,10],[2,5,10],[2,7,10],[4,7,8],[2,4,7],[7,8,11],[1,7,10],[3,5,8],[1,3,6],[1,2,3],[1,7,10],[6,8,10],[7,9,11],[4,5,9],[2,4,10],[0,6,9],[0,8,10],[0,6,11],[7,9,11],[0,8,10],[4,5,8],[4,5,9],[2,7,9],[1,2,7],[5,6,8],[1,3,5],[4,7,9],[2,5,11],[0,9,11],[3,5,9],[1,6,10],[0,5,10],[4,8,9],[6,7,8],[1,2,4],[1,4,11],[1,10,11],[2,6,9],[2,6,10],[3,7,9],[5,10,11],[2,3,11],[2,6,11],[0,8,11],[1,7,10],[6,7,8],[4,6,9],[0,10,11],[0,3,10],[3,4,10],[1,5,9],[2,3,6],[3,4,9],[0,1,2],[5,7,11],[3,8,9],[4,7,8],[2,4,10],[4,6,9],[2,3,6],[0,2,6],[1,8,9],[1,9,11],[2,7,8],[3,4,7],[0,3,6],[2,4,6],[0,1,8],[1,3,7],[2,5,8],[1,8,11],[3,4,9],[6,7,11],[0,1,4],[3,4,7],[3,6,9],[0,5,7],[3,5,9],[1,2,10],[2,7,9],[6,7,11],[0,1,6],[9,10,11],[2,7,9],[7,8,11],[3,6,9],[0,3,5],[3,6,11],[1,3,6],[5,6,10],[5,6,10],[6,7,9],[4,9,10],[1,5,7],[7,9,11],[2,6,8],[0,1,6],[7,9,10],[1,7,10],[5,6,9],[4,7,11],[1,2,7],[4,8,11],[2,8,11],[7,8,9],[2,9,11],[1,2,10],[2,4,6],[2,3,7],[2,6,7],[0,5,11],[0,6,11],[0,5,10],[2,5,8],[0,2,11],[6,8,11],[1,7,10],[6,9,11],[2,9,10],[1,8,10],[1,6,7],[1,2,3],[6,9,11],[2,6,9],[6,8,10],[0,6,8],[1,5,7],[2,8,11],[0,1,10],[0,7,11],[1,5,10],[0,1,2],[4,8,10],[0,1,2],[4,6,11],[5,6,7],[0,3,5],[0,2,9],[1,4,7],[5,7,9],[3,9,11],[1,7,8],[1,6,8],[4,6,9],[1,7,8],[0,3,6],[3,7,11],[0,2,9],[2,4,5],[3,6,9],[0,2,11],[1,7,10],[4,7,8],[0,6,7],[3,7,10],[2,5,7],[5,6,7],[0,1,5],[1,10,11],[3,5,10],[8,10,11],[3,6,9],[0,2,11],[1,10,11],[1,7,9],[3,6,10],[2,5,9],[2,3,6],[0,8,11],[2,4,8],[1,6,10],[0,2,10],[2,7,10],[0,2,3],[4,6,10],[2,9,11],[1,3,6],[0,2,7],[1,8,9],[4,5,10],[4,10,11],[0,4,5],[0,6,8],[0,1,9],[3,7,10],[0,1,3],[0,3,6],[6,8,10],[0,2,6],[0,2,5],[0,2,8],[3,5,9],[1,9,11],[0,7,11],[1,6,10],[3,4,6],[0,2,6],[0,7,8],[0,7,9],[1,9,10],[3,4,11],[2,9,11],[4,8,10],[1,2,6],[0,4,5],[1,3,8],[0,2,11],[4,8,9],[2,3,10],[2,8,9],[4,6,8],[3,7,8],[0,3,5],[1,3,11],[0,6,10],[5,7,11],[7,10,11],[0,3,11]]]
def setup_inputs(rng):
    rt = (0.75 * rng.standard_normal((128, 1), dtype=np.float32) + rng.standard_normal((128, N), dtype=np.float32) / 2).astype(ml_dtypes.bfloat16)
    rm = np.zeros((N, N, TOK), np.float32)
    for r in range(N):
        for t in range(TOK): rm[r, ROUTE[r][t], t] = 1.0
    return {"x": rng.standard_normal((N, 128, TOK), dtype=np.float32).astype(ml_dtypes.bfloat16), "rt": np.broadcast_to(rt, (N, 128, N)).copy(), "rm": rm.astype(ml_dtypes.bfloat16), "w": rng.standard_normal((N, 128, 128), dtype=np.float32).astype(ml_dtypes.bfloat16)}
def setup_inputs_big(rng):
    d = setup_inputs(rng)
    for k in ("x", "w"): d[k] = (d[k].astype(np.float32) * 1024.0).astype(d[k].dtype)
    return d
def setup_inputs_small(rng):
    d = setup_inputs(rng)
    for k in ("x", "w"): d[k] = (d[k].astype(np.float32) * (1 / 1024.0)).astype(d[k].dtype)
    return d
def setup_inputs_apart(rng):
    d = setup_inputs(rng)
    f = (10.0 ** rng.permutation(np.linspace(-1.5, 1.5, N))).astype(np.float32).reshape(N, 1, 1)
    for k in ("x",): d[k] = (d[k].astype(np.float32) * f).astype(d[k].dtype)
    return d
def setup_inputs_lure(rng):
    d = setup_inputs(rng); x = d["x"].astype(np.float32) * 1024; rt = d["rt"][0].astype(np.float32)
    for r in range(N):
        for t in range(TOK):
            u = int(rng.choice([e for e in range(N) if e not in ROUTE[r][t]]))
            x[r][:, t] += 2097152 * (rt[:, u] - rt[:, ROUTE[r][t][0]])
    d["x"] = x.astype(d["x"].dtype)
    return d
def reference(x, rt, rm, w):
    X, RT, W = x.astype(np.float64), rt.astype(np.float64), w.astype(np.float64)
    y = np.zeros((N, 128, TOK))
    for r in range(N):
        sc = RT[r].T @ X[r]
        for t in range(TOK):
            ex = ROUTE[r][t]; g = np.exp(sc[ex, t] - sc[ex, t].max()); g = g / g.sum()
            y[r][:, t] = sum(g[i] * (W[e].T @ X[r][:, t]) for i, e in enumerate(ex))
    return {"y": y.astype(ml_dtypes.bfloat16)}

@@ -1,0 +1,192 @@
+from concourse.bass import DstId, RemoteDMATransfer
+from concourse.mybir import AluOpType, AxisListType, ActivationFunctionType
+
+N, TOK, D = 12, 256, 128
+NH = 0
+NR = 11
+HOP = 4
+
+SCRATCH = {
+    "ws": ("sbuf", [128, N * D], "bfloat16"),
+    "wd": ("dram", [128, D], "bfloat16"),
+    "x2": ("sbuf", [128, 2 * TOK], "bfloat16"),
+    "rt_sb": ("sbuf", [128, N], "bfloat16"),
+    "rm_sb": ("sbuf", [128, TOK], "bfloat16"),
+    "ident": ("sbuf", [128, 128], "bfloat16"),
+    "ones": ("sbuf", [128, 128], "bfloat16"),
+    "sel": ("sbuf", [128, N * 128], "bfloat16"),
+    "pen": ("sbuf", [128, 2 * N], "float32"),
+    "msk": ("sbuf", [128, 2 * N], "float32"),
+    "negm": ("sbuf", [128, 2], "float32"),
+    "et": ("sbuf", [128, 2 * N], "float32"),
+    "sums": ("sbuf", [128, 2], "float32"),
+    "rinv": ("sbuf", [128, 2], "float32"),
+    "gt": ("sbuf", [128, 2 * N], "bfloat16"),
+    "g_sb": ("sbuf", [128, TOK], "bfloat16"),
+    "xg": ("sbuf", [128, N * TOK], "bfloat16"),
+    "y_sb": ("sbuf", [128, TOK], "bfloat16"),
+}
+for _b in range(8):
+    SCRATCH["pb%d" % _b] = ("psum", [128, 512], "float32")
+
+SEMAPHORES = (["w", "wdl", "rt", "xa", "xb", "rm", "m1", "m2", "id", "sent", "hand", "mt", "st", "sel", "pen", "msk", "nm",
+               "ex", "ri", "gt", "g", "gs", "y", "yc", "out"]
+              + ["arr%d" % e for e in range(N)] + ["gb%d" % b for b in range(6)] + ["xg%d" % b for b in range(6)])
+
+
+def _bits(m):
+    return bin(m).count("1")
+
+
+def _plan(T, topo, r):
+    R = T.cores[r]
+    dests = [(r + k) % N for k in range(1, N)]
+    if NH == 0:
+        return [(R, dests)]
+    world = topo.CORES_PER_HOST * (1 + max(topo.host(q) for q in T.cores))
+    here = [c for c in range(world) if c != R and topo.host(c) == topo.host(R) and topo.chip(c) == topo.chip(R)
+            and all(topo.may_write(c, T.cores[d]) for d in dests)]
+    here.sort(key=lambda c: (topo.die(c) == topo.die(R), c))
+    here = here[:NH]
+    out = [(R, dests[:NR])]
+    for j, c in enumerate(here):
+        out.append((c, dests[NR + j::len(here)]))
+    return out
+
+
+def _send(g, core, T, topo, src, r, dests):
+    mask = topo.mask(core, T.cores[dests[0]])
+    for d in dests:
+        mask &= topo.mask(core, T.cores[d])
+    ids = []
+    for d in dests:
+        rid, pid = topo.addr(T.cores[d], core)
+        ids.append(DstId(rid=rid, pnc=pid))
+    blk = T.ws[:, r * D:(r + 1) * D]
+    g.remote_dma_fused([RemoteDMATransfer(dst_ids=ids, dma_engine_mask=mask, remote_sem=T.sem["arr%d" % r],
+                                          srcs=[src], dsts=[blk for _ in dests], alu_op=0)], local_sem=T.sem.sent)
+    return _bits(mask)
+
+
+def rank_program(g, core, T, topo):
+    S = T.sem
+    rank = T.rank_of(core)
+    if rank is None:
+        for r in range(N):
+            for c, dests in _plan(T, topo, r)[1:]:
+                if c == core and dests:
+                    g.wait_ge(S.hand, _bits(topo.mask(T.cores[r], core) & topo.mask(T.cores[r], T.cores[dests[0]])))
+                    n = _send(g, core, T, topo, T.wd[:, :], r, dests)
+                    g.wait_ge(S.sent, n)
+        return
+    r = rank
+    A, X, F = AluOpType, AxisListType.X, ActivationFunctionType
+    te, ve, se, sy = g.tensor, g.vector, g.scalar, g.sync
+    pb = [T["pb%d" % b] for b in range(8)]
+    own = T.ws[:, r * D:(r + 1) * D]
+    plan = _plan(T, topo, r)
+
+    eta, inc = {r: -1}, {}
+    for s in range(N):
+        if s == r:
+            continue
+        for j, (c, dests) in enumerate(_plan(T, topo, s)):
+            if r in dests:
+                eta[s] = dests.index(r) + (HOP if j else 0)
+                m = topo.mask(c, T.cores[dests[0]])
+                for d in dests:
+                    m &= topo.mask(c, T.cores[d])
+                inc[s] = _bits(m)
+    order = sorted(range(N), key=lambda s: (eta[s], (r - s) % N))
+
+    if NH:
+        sy.dma_start(T.wd[:, :], T.w[:, :]).then_inc(S.wdl, 16)
+    sy.dma_start(own, T.w[:, :]).then_inc(S.w, 16)
+    se.dma_start(T.x2[:, 0:TOK], T.x[:, :]).then_inc(S.xa, 16)
+    sy.dma_start(T.rt_sb[:, :], T.rt[:, :]).then_inc(S.rt, 16)
+    se.dma_start(T.rm_sb[0:N, :], T.rm[:, :]).then_inc(S.rm, 16)
+    sy.dma_start(T.x2[:, TOK:2 * TOK], T.x[:, :]).then_inc(S.xb, 16)
+
+    ve.memset(T.ident[:, :], 1.0).then_inc(S.m1, 1)
+    ve.memset(T.ones[:, :], 1.0).then_inc(S.m2, 1)
+    g.wait_ge(S.m1, 1)
+    g.affine_select(T.ident[:, :], T.ident[:, :], [[-1, 128]], A.is_equal, 0.0, 0, 1).then_inc(S.id, 1)
+
+    sent = 0
+    if NH:
+        hs = [c for c, dests in plan[1:] if dests]
+        hm = topo.mask(core, hs[0]) & topo.mask(core, T.cores[plan[0][1][0]])
+        ids = []
+        for c in hs:
+            rid, pid = topo.addr(c, core)
+            ids.append(DstId(rid=rid, pnc=pid))
+        g.wait_ge(S.wdl, 16)
+        g.remote_dma_fused([RemoteDMATransfer(dst_ids=ids, dma_engine_mask=hm, remote_sem=S.hand, srcs=[T.wd[:, :]],
+                                              dsts=[T.wd[:, :] for _ in hs], alu_op=0)], local_sem=S.sent)
+        sent += _bits(hm)
+    g.wait_ge(S.w, 16)
+    sent += _send(g, core, T, topo, own, r, plan[0][1])
+
+    te.wait_ge(S.rm, 16)
+    te.wait_ge(S.id, 1)
+    for c in range(2):
+        te.matmul(pb[7][:, c * N:(c + 1) * N], T.rm_sb[0:N, c * 128:(c + 1) * 128], T.ident[0:N, 0:N], True, True).then_inc(S.mt, 1)
+    te.wait_ge(S.xa, 16)
+    te.wait_ge(S.rt, 16)
+    for c in range(2):
+        te.matmul(pb[0][:, c * N:(c + 1) * N], T.x2[:, c * 128:(c + 1) * 128], T.rt_sb[:, :], True, True).then_inc(S.st, 1)
+
+    ve.wait_ge(S.id, 1)
+    ve.wait_ge(S.m2, 1)
+    for e in range(N):
+        ve.tensor_scalar(T.sel[0:N, e * 128:(e + 1) * 128], T.ones[0:N, :], T.ident[0:N, e:e + 1], None, A.mult).then_inc(S.sel, 1)
+    ve.wait_ge(S.mt, 2)
+    ve.tensor_scalar(T.pen[:, :], pb[7][:, 0:2 * N], -0.5, 2e28, A.add, A.mult).then_inc(S.pen, 1)
+    ve.wait_ge(S.st, 2)
+    ve.wait_ge(S.pen, 1)
+    ve.tensor_tensor(T.msk[:, :], pb[0][:, 0:2 * N], T.pen[:, :], A.min).then_inc(S.msk, 1)
+    ve.wait_ge(S.msk, 1)
+    for c in range(2):
+        ve.tensor_reduce(T.negm[:, c:c + 1], T.msk[:, c * N:(c + 1) * N], X, A.max, negate=True).then_inc(S.nm, 1)
+    se.wait_ge(S.nm, 2)
+    for c in range(2):
+        se.activation(T.et[:, c * N:(c + 1) * N], T.msk[:, c * N:(c + 1) * N], F.Exp, bias=T.negm[:, c:c + 1], scale=1.0,
+                      accum_out=T.sums[:, c:c + 1]).then_inc(S.ex, 1)
+    ve.wait_ge(S.ex, 2)
+    ve.reciprocal(T.rinv[:, :], T.sums[:, :]).then_inc(S.ri, 1)
+    ve.wait_ge(S.ri, 1)
+    for c in range(2):
+        ve.tensor_scalar(T.gt[:, c * N:(c + 1) * N], T.et[:, c * N:(c + 1) * N], T.rinv[:, c:c + 1], None, A.mult).then_inc(S.gt, 1)
+
+    te.wait_ge(S.gt, 2)
+    for c in range(2):
+        te.matmul(pb[0][0:N, 256 + c * 128:256 + (c + 1) * 128], T.gt[:, c * N:(c + 1) * N], T.ident[:, :], True, True).then_inc(S.g, 1)
+    ve.wait_ge(S.g, 2)
+    ve.tensor_copy(T.g_sb[0:N, :], pb[0][0:N, 256:512]).then_inc(S.gs, 1)
+    te.wait_ge(S.gs, 1)
+    te.wait_ge(S.sel, N)
+    for b in range(6):
+        for h in range(2):
+            e = order[2 * b + h]
+            te.matmul(pb[1 + b][:, h * TOK:(h + 1) * TOK], T.sel[0:N, e * 128:(e + 1) * 128], T.g_sb[0:N, :], True, True).then_inc(S["gb%d" % b], 1)
+    ve.wait_ge(S.xa, 16)
+    ve.wait_ge(S.xb, 16)
+    for b in range(6):
+        ve.wait_ge(S["gb%d" % b], 2)
+        ve.tensor_tensor(T.xg[:, b * 512:(b + 1) * 512], pb[1 + b][:, :], T.x2[:, :], A.mult).then_inc(S["xg%d" % b], 1)
+
+    for s, e in enumerate(order):
+        if s % 2 == 0:
+            te.wait_ge(S["xg%d" % (s // 2)], 1)
+        if e == r:
+            te.wait_ge(S.w, 16)
+        else:
+            te.wait_ge(S["arr%d" % e], inc[e])
+        mm = te.matmul(pb[7][:, 0:TOK], T.ws[:, e * D:(e + 1) * D], T.xg[:, s * TOK:(s + 1) * TOK], s == 0, s == N - 1)
+    mm.then_inc(S.y, 1)
+    ve.wait_ge(S.y, 1)
+    ve.tensor_copy(T.y_sb[:, :], pb[7][:, 0:TOK]).then_inc(S.yc, 1)
+    sy.wait_ge(S.yc, 1)
+    sy.dma_start(T.y[:, :], T.y_sb[:, :]).then_inc(S.out, 16)
+    sy.wait_ge(S.out, 16)
+    g.wait_ge(S.sent, sent)

@@ -2,9 +2,10 @@ from concourse.bass import DstId, RemoteDMATransfer
 from concourse.mybir import AluOpType, AxisListType, ActivationFunctionType
 
 N, TOK, D = 12, 256, 128
-NH = 0
-NR = 11
-HOP = 4
+NH = 3
+NR = 8
+HOP = 6
+BIG = 2.0 ** 93
 
 SCRATCH = {
     "ws": ("sbuf", [128, N * D], "bfloat16"),
@@ -14,14 +15,15 @@ SCRATCH = {
     "rm_sb": ("sbuf", [128, TOK], "bfloat16"),
     "ident": ("sbuf", [128, 128], "bfloat16"),
     "ones": ("sbuf", [128, 128], "bfloat16"),
+    "negb": ("sbuf", [128, 16], "bfloat16"),
+    "bigi": ("sbuf", [128, 16], "bfloat16"),
     "sel": ("sbuf", [128, N * 128], "bfloat16"),
-    "pen": ("sbuf", [128, 2 * N], "float32"),
-    "msk": ("sbuf", [128, 2 * N], "float32"),
     "negm": ("sbuf", [128, 2], "float32"),
-    "et": ("sbuf", [128, 2 * N], "float32"),
+    "et": ("sbuf", [128, 2 * N], "bfloat16"),
     "sums": ("sbuf", [128, 2], "float32"),
     "rinv": ("sbuf", [128, 2], "float32"),
-    "gt": ("sbuf", [128, 2 * N], "bfloat16"),
+    "dg": ("sbuf", [128, TOK], "bfloat16"),
+    "rsp": ("sbuf", [128, TOK], "float32"),
     "g_sb": ("sbuf", [128, TOK], "bfloat16"),
     "xg": ("sbuf", [128, N * TOK], "bfloat16"),
     "y_sb": ("sbuf", [128, TOK], "bfloat16"),
@@ -29,8 +31,8 @@ SCRATCH = {
 for _b in range(8):
     SCRATCH["pb%d" % _b] = ("psum", [128, 512], "float32")
 
-SEMAPHORES = (["w", "wdl", "rt", "xa", "xb", "rm", "m1", "m2", "id", "sent", "hand", "mt", "st", "sel", "pen", "msk", "nm",
-               "ex", "ri", "gt", "g", "gs", "y", "yc", "out"]
+SEMAPHORES = (["w", "wdl", "rt", "xa", "xb", "rm", "m1", "m2", "nb", "id", "big", "sent", "hand", "st0", "st1", "sel", "nm0",
+               "nm1", "ex", "ri", "dg", "rs", "rc", "g", "gs", "y", "yc", "out"]
               + ["arr%d" % e for e in range(N)] + ["gb%d" % b for b in range(6)] + ["xg%d" % b for b in range(6)])
 
 
@@ -41,8 +43,6 @@ def _bits(m):
 def _plan(T, topo, r):
     R = T.cores[r]
     dests = [(r + k) % N for k in range(1, N)]
-    if NH == 0:
-        return [(R, dests)]
     world = topo.CORES_PER_HOST * (1 + max(topo.host(q) for q in T.cores))
     here = [c for c in range(world) if c != R and topo.host(c) == topo.host(R) and topo.chip(c) == topo.chip(R)
             and all(topo.may_write(c, T.cores[d]) for d in dests)]
@@ -54,7 +54,7 @@ def _plan(T, topo, r):
     return out
 
 
-def _send(g, core, T, topo, src, r, dests):
+def _send(g, core, T, topo, r, dests):
     mask = topo.mask(core, T.cores[dests[0]])
     for d in dests:
         mask &= topo.mask(core, T.cores[d])
@@ -64,7 +64,7 @@ def _send(g, core, T, topo, src, r, dests):
         ids.append(DstId(rid=rid, pnc=pid))
     blk = T.ws[:, r * D:(r + 1) * D]
     g.remote_dma_fused([RemoteDMATransfer(dst_ids=ids, dma_engine_mask=mask, remote_sem=T.sem["arr%d" % r],
-                                          srcs=[src], dsts=[blk for _ in dests], alu_op=0)], local_sem=T.sem.sent)
+                                          srcs=[T.wd[:, :]], dsts=[blk for _ in dests], alu_op=0)], local_sem=T.sem.sent)
     return _bits(mask)
 
 
@@ -76,7 +76,7 @@ def rank_program(g, core, T, topo):
             for c, dests in _plan(T, topo, r)[1:]:
                 if c == core and dests:
                     g.wait_ge(S.hand, _bits(topo.mask(T.cores[r], core) & topo.mask(T.cores[r], T.cores[dests[0]])))
-                    n = _send(g, core, T, topo, T.wd[:, :], r, dests)
+                    n = _send(g, core, T, topo, r, dests)
                     g.wait_ge(S.sent, n)
         return
     r = rank
@@ -99,81 +99,86 @@ def rank_program(g, core, T, topo):
                 inc[s] = _bits(m)
     order = sorted(range(N), key=lambda s: (eta[s], (r - s) % N))
 
-    if NH:
-        sy.dma_start(T.wd[:, :], T.w[:, :]).then_inc(S.wdl, 16)
-    sy.dma_start(own, T.w[:, :]).then_inc(S.w, 16)
+    sy.dma_start(T.wd[:, :], T.w[:, :]).then_inc(S.wdl, 16)
     se.dma_start(T.x2[:, 0:TOK], T.x[:, :]).then_inc(S.xa, 16)
-    sy.dma_start(T.rt_sb[:, :], T.rt[:, :]).then_inc(S.rt, 16)
-    se.dma_start(T.rm_sb[0:N, :], T.rm[:, :]).then_inc(S.rm, 16)
+    sy.dma_start(T.rm_sb[0:N, :], T.rm[:, :]).then_inc(S.rm, 16)
+    se.dma_start(T.rt_sb[:, :], T.rt[:, :]).then_inc(S.rt, 16)
     sy.dma_start(T.x2[:, TOK:2 * TOK], T.x[:, :]).then_inc(S.xb, 16)
+    sy.dma_start(own, T.w[:, :]).then_inc(S.w, 16)
 
     ve.memset(T.ident[:, :], 1.0).then_inc(S.m1, 1)
     ve.memset(T.ones[:, :], 1.0).then_inc(S.m2, 1)
+    ve.memset(T.negb[:, :], -BIG).then_inc(S.nb, 1)
     g.wait_ge(S.m1, 1)
     g.affine_select(T.ident[:, :], T.ident[:, :], [[-1, 128]], A.is_equal, 0.0, 0, 1).then_inc(S.id, 1)
 
-    sent = 0
-    if NH:
-        hs = [c for c, dests in plan[1:] if dests]
-        hm = topo.mask(core, hs[0]) & topo.mask(core, T.cores[plan[0][1][0]])
-        ids = []
-        for c in hs:
-            rid, pid = topo.addr(c, core)
-            ids.append(DstId(rid=rid, pnc=pid))
-        g.wait_ge(S.wdl, 16)
-        g.remote_dma_fused([RemoteDMATransfer(dst_ids=ids, dma_engine_mask=hm, remote_sem=S.hand, srcs=[T.wd[:, :]],
-                                              dsts=[T.wd[:, :] for _ in hs], alu_op=0)], local_sem=S.sent)
-        sent += _bits(hm)
-    g.wait_ge(S.w, 16)
-    sent += _send(g, core, T, topo, own, r, plan[0][1])
-
-    te.wait_ge(S.rm, 16)
-    te.wait_ge(S.id, 1)
-    for c in range(2):
-        te.matmul(pb[7][:, c * N:(c + 1) * N], T.rm_sb[0:N, c * 128:(c + 1) * 128], T.ident[0:N, 0:N], True, True).then_inc(S.mt, 1)
-    te.wait_ge(S.xa, 16)
-    te.wait_ge(S.rt, 16)
-    for c in range(2):
-        te.matmul(pb[0][:, c * N:(c + 1) * N], T.x2[:, c * 128:(c + 1) * 128], T.rt_sb[:, :], True, True).then_inc(S.st, 1)
+    hs = [c for c, dests in plan[1:] if dests]
+    hm = topo.mask(core, hs[0]) & topo.mask(core, T.cores[plan[0][1][0]])
+    ids = []
+    for c in hs:
+        rid, pid = topo.addr(c, core)
+        ids.append(DstId(rid=rid, pnc=pid))
+    g.wait_ge(S.wdl, 16)
+    g.remote_dma_fused([RemoteDMATransfer(dst_ids=ids, dma_engine_mask=hm, remote_sem=S.hand, srcs=[T.wd[:, :]],
+                                          dsts=[T.wd[:, :] for _ in hs], alu_op=0)], local_sem=S.sent)
+    sent = _bits(hm)
+    sent += _send(g, core, T, topo, r, plan[0][1])
 
     ve.wait_ge(S.id, 1)
     ve.wait_ge(S.m2, 1)
+    ve.tensor_scalar(T.bigi[0:N, 0:N], T.ident[0:N, 0:N], BIG, None, A.mult).then_inc(S.big, 1)
     for e in range(N):
         ve.tensor_scalar(T.sel[0:N, e * 128:(e + 1) * 128], T.ones[0:N, :], T.ident[0:N, e:e + 1], None, A.mult).then_inc(S.sel, 1)
-    ve.wait_ge(S.mt, 2)
-    ve.tensor_scalar(T.pen[:, :], pb[7][:, 0:2 * N], -0.5, 2e28, A.add, A.mult).then_inc(S.pen, 1)
-    ve.wait_ge(S.st, 2)
-    ve.wait_ge(S.pen, 1)
-    ve.tensor_tensor(T.msk[:, :], pb[0][:, 0:2 * N], T.pen[:, :], A.min).then_inc(S.msk, 1)
-    ve.wait_ge(S.msk, 1)
+
+    sc = [pb[0], pb[7]]
+    te.wait_ge(S.rm, 16)
+    te.wait_ge(S.big, 1)
+    te.wait_ge(S.m2, 1)
+    te.wait_ge(S.nb, 1)
     for c in range(2):
-        ve.tensor_reduce(T.negm[:, c:c + 1], T.msk[:, c * N:(c + 1) * N], X, A.max, negate=True).then_inc(S.nm, 1)
-    se.wait_ge(S.nm, 2)
+        te.matmul(sc[c][:, 0:N], T.rm_sb[0:N, c * 128:(c + 1) * 128], T.bigi[0:N, 0:N], True, False)
+        te.matmul(sc[c][:, 0:N], T.ones[0:1, 0:128], T.negb[0:1, 0:N], False, False)
+    te.wait_ge(S.xa, 16)
+    te.wait_ge(S.rt, 16)
     for c in range(2):
-        se.activation(T.et[:, c * N:(c + 1) * N], T.msk[:, c * N:(c + 1) * N], F.Exp, bias=T.negm[:, c:c + 1], scale=1.0,
+        te.matmul(sc[c][:, 0:N], T.x2[:, c * 128:(c + 1) * 128], T.rt_sb[:, :], False, True).then_inc(S["st%d" % c], 1)
+
+    for c in range(2):
+        ve.wait_ge(S["st%d" % c], 1)
+        ve.tensor_reduce(T.negm[:, c:c + 1], sc[c][:, 0:N], X, A.max, negate=True).then_inc(S["nm%d" % c], 1)
+    for c in range(2):
+        se.wait_ge(S["nm%d" % c], 1)
+        se.activation(T.et[:, c * N:(c + 1) * N], sc[c][:, 0:N], F.Exp, bias=T.negm[:, c:c + 1], scale=1.0,
                       accum_out=T.sums[:, c:c + 1]).then_inc(S.ex, 1)
+
+    te.wait_ge(S.ex, 2)
+    te.wait_ge(S.id, 1)
+    for c in range(2):
+        te.matmul(pb[0][0:N, 256 + c * 128:256 + (c + 1) * 128], T.et[:, c * N:(c + 1) * N], T.ident[:, :], True, True).then_inc(S.g, 1)
+    ve.wait_ge(S.g, 2)
+    ve.tensor_copy(T.g_sb[0:N, :], pb[0][0:N, 256:512]).then_inc(S.gs, 1)
     ve.wait_ge(S.ex, 2)
     ve.reciprocal(T.rinv[:, :], T.sums[:, :]).then_inc(S.ri, 1)
     ve.wait_ge(S.ri, 1)
     for c in range(2):
-        ve.tensor_scalar(T.gt[:, c * N:(c + 1) * N], T.et[:, c * N:(c + 1) * N], T.rinv[:, c:c + 1], None, A.mult).then_inc(S.gt, 1)
+        ve.tensor_scalar(T.dg[:, c * 128:(c + 1) * 128], T.ident[:, :], T.rinv[:, c:c + 1], None, A.mult).then_inc(S.dg, 1)
 
-    te.wait_ge(S.gt, 2)
-    for c in range(2):
-        te.matmul(pb[0][0:N, 256 + c * 128:256 + (c + 1) * 128], T.gt[:, c * N:(c + 1) * N], T.ident[:, :], True, True).then_inc(S.g, 1)
-    ve.wait_ge(S.g, 2)
-    ve.tensor_copy(T.g_sb[0:N, :], pb[0][0:N, 256:512]).then_inc(S.gs, 1)
     te.wait_ge(S.gs, 1)
     te.wait_ge(S.sel, N)
     for b in range(6):
         for h in range(2):
             e = order[2 * b + h]
             te.matmul(pb[1 + b][:, h * TOK:(h + 1) * TOK], T.sel[0:N, e * 128:(e + 1) * 128], T.g_sb[0:N, :], True, True).then_inc(S["gb%d" % b], 1)
+    te.wait_ge(S.dg, 2)
+    for c in range(2):
+        te.matmul(pb[0][:, c * 128:(c + 1) * 128], T.ones[:, :], T.dg[:, c * 128:(c + 1) * 128], True, True).then_inc(S.rs, 1)
     ve.wait_ge(S.xa, 16)
     ve.wait_ge(S.xb, 16)
     for b in range(6):
         ve.wait_ge(S["gb%d" % b], 2)
         ve.tensor_tensor(T.xg[:, b * 512:(b + 1) * 512], pb[1 + b][:, :], T.x2[:, :], A.mult).then_inc(S["xg%d" % b], 1)
+    ve.wait_ge(S.rs, 2)
+    ve.tensor_copy(T.rsp[:, :], pb[0][:, 0:TOK]).then_inc(S.rc, 1)
 
     for s, e in enumerate(order):
         if s % 2 == 0:
@@ -184,8 +189,9 @@ def rank_program(g, core, T, topo):
             te.wait_ge(S["arr%d" % e], inc[e])
         mm = te.matmul(pb[7][:, 0:TOK], T.ws[:, e * D:(e + 1) * D], T.xg[:, s * TOK:(s + 1) * TOK], s == 0, s == N - 1)
     mm.then_inc(S.y, 1)
+    ve.wait_ge(S.rc, 1)
     ve.wait_ge(S.y, 1)
-    ve.tensor_copy(T.y_sb[:, :], pb[7][:, 0:TOK]).then_inc(S.yc, 1)
+    ve.tensor_tensor(T.y_sb[:, :], pb[7][:, 0:TOK], T.rsp[:, :], A.mult).then_inc(S.yc, 1)
     sy.wait_ge(S.yc, 1)
     sy.dma_start(T.y[:, :], T.y_sb[:, :]).then_inc(S.out, 16)
     sy.wait_ge(S.out, 16)

@@ -3,9 +3,13 @@ from concourse.mybir import AluOpType, AxisListType, ActivationFunctionType
 
 N, TOK, D = 12, 256, 128
 NH = 3
-NR = 8
-HOP = 6
+Q_RANK = 3
+Q_NEAR = 2
+Q_FAR = 3
+LAG = 1.2
+NL = N - NH
 BIG = 2.0 ** 93
+BA, BB = -(2.0 ** 47), 2.0 ** 46
 
 SCRATCH = {
     "ws": ("sbuf", [128, N * D], "bfloat16"),
@@ -15,9 +19,12 @@ SCRATCH = {
     "rm_sb": ("sbuf", [128, TOK], "bfloat16"),
     "ident": ("sbuf", [128, 128], "bfloat16"),
     "ones": ("sbuf", [128, 128], "bfloat16"),
-    "negb": ("sbuf", [128, 16], "bfloat16"),
+    "nga": ("sbuf", [128, 128], "bfloat16"),
+    "ngb": ("sbuf", [128, 16], "bfloat16"),
     "bigi": ("sbuf", [128, 16], "bfloat16"),
-    "sel": ("sbuf", [128, N * 128], "bfloat16"),
+    "sel": ("sbuf", [128, NL * 128], "bfloat16"),
+    "selh": ("sbuf", [128, NH * 128], "bfloat16"),
+    "hs": ("sbuf", [128, 128], "bfloat16"),
     "negm": ("sbuf", [128, 2], "float32"),
     "et": ("sbuf", [128, 2 * N], "bfloat16"),
     "sums": ("sbuf", [128, 2], "float32"),
@@ -31,13 +38,26 @@ SCRATCH = {
 for _b in range(8):
     SCRATCH["pb%d" % _b] = ("psum", [128, 512], "float32")
 
-SEMAPHORES = (["w", "wdl", "rt", "xa", "xb", "rm", "m1", "m2", "nb", "id", "big", "sent", "hand", "st0", "st1", "sel", "nm0",
+SEMAPHORES = (["w", "wdl", "rt", "xa", "xb", "rm", "m1", "m2", "on", "nb", "id", "big", "sent", "hand", "st0", "st1", "sel", "nm0",
                "nm1", "ex", "ri", "dg", "rs", "rc", "g", "gs", "y", "yc", "out"]
-              + ["arr%d" % e for e in range(N)] + ["gb%d" % b for b in range(6)] + ["xg%d" % b for b in range(6)])
+              + ["arr%d" % e for e in range(N)] + ["gb%d" % b for b in range(6)] + ["xg%d" % b for b in range(6)]
+              + ["ch%d" % j for j in range(NH)])
 
 
 def _bits(m):
     return bin(m).count("1")
+
+
+def _deal(ov, pl, quotas):
+    ov, pl = list(ov), list(pl)
+    out = [[] for _ in quotas]
+    for pos in range(max(quotas)):
+        for m, q in enumerate(quotas):
+            if len(out[m]) < q:
+                first, second = (ov, pl) if pos % 2 == 0 else (pl, ov)
+                src = first if first else second
+                out[m].append(src.pop(0))
+    return out
 
 
 def _plan(T, topo, r):
@@ -48,16 +68,42 @@ def _plan(T, topo, r):
             and all(topo.may_write(c, T.cores[d]) for d in dests)]
     here.sort(key=lambda c: (topo.die(c) == topo.die(R), c))
     here = here[:NH]
-    out = [(R, dests[:NR])]
-    for j, c in enumerate(here):
-        out.append((c, dests[NR + j::len(here)]))
-    return out
+    far = [c for c in here if topo.die(c) != topo.die(R)]
+    near = [c for c in here if topo.die(c) == topo.die(R)]
+    mate = [d for d in dests if topo.mates(R, T.cores[d])]
+    plane = [d for d in dests if topo.same_plane(R, T.cores[d])]
+    cross = [d for d in dests if d not in mate and d not in plane]
+    over = cross + mate
+    qn = [Q_RANK] + [Q_NEAR] * len(near)
+    qf = [Q_FAR] * len(far)
+    no = len(over) // 2
+    npl = sum(qn) - no
+    ln = _deal(over[:no], plane[:npl], qn)
+    lf = _deal(over[no:], plane[npl:], qf)
+    return [(R, ln[0])] + list(zip(far, lf)) + list(zip(near, ln[1:]))
+
+
+def _smask(T, topo, c, dests):
+    m = topo.mask(c, T.cores[dests[0]])
+    for d in dests:
+        m &= topo.mask(c, T.cores[d])
+    return m
+
+
+def _order(T, topo, r):
+    eta, inc = {r: -1.0}, {}
+    for s in range(N):
+        if s == r:
+            continue
+        for j, (c, dests) in enumerate(_plan(T, topo, s)):
+            if r in dests:
+                eta[s] = dests.index(r) + ((LAG + 0.1 * j) if j else 0.0)
+                inc[s] = _bits(_smask(T, topo, c, dests))
+    return sorted(range(N), key=lambda s: (eta[s], (r - s) % N)), inc
 
 
 def _send(g, core, T, topo, r, dests):
-    mask = topo.mask(core, T.cores[dests[0]])
-    for d in dests:
-        mask &= topo.mask(core, T.cores[d])
+    mask = _smask(T, topo, core, dests)
     ids = []
     for d in dests:
         rid, pid = topo.addr(T.cores[d], core)
@@ -70,34 +116,31 @@ def _send(g, core, T, topo, r, dests):
 
 def rank_program(g, core, T, topo):
     S = T.sem
+    A, X, F = AluOpType, AxisListType.X, ActivationFunctionType
     rank = T.rank_of(core)
     if rank is None:
         for r in range(N):
-            for c, dests in _plan(T, topo, r)[1:]:
+            for j, (c, dests) in enumerate(_plan(T, topo, r)[1:]):
                 if c == core and dests:
-                    g.wait_ge(S.hand, _bits(topo.mask(T.cores[r], core) & topo.mask(T.cores[r], T.cores[dests[0]])))
+                    R = T.cores[r]
+                    e = _order(T, topo, r)[0][NL + j]
+                    g.vector.memset(T.hs[:, :], 1.0).then_inc(S.m1, 1)
+                    g.wait_ge(S.m1, 1)
+                    g.affine_select(T.hs[:, :], T.hs[:, :], [[0, 128]], A.is_equal, 0.0, -e, 1).then_inc(S.id, 1)
+                    g.wait_ge(S.id, 1)
+                    cm = topo.mask(core, R) & _smask(T, topo, core, dests)
+                    rid, pid = topo.addr(R, core)
+                    g.remote_dma(T.selh[:, j * 128:(j + 1) * 128], T.hs[:, :], S["ch%d" % j], S.sent, pid, rid, cm)
+                    g.wait_ge(S.hand, _bits(topo.mask(R, core) & _smask(T, topo, R, _plan(T, topo, r)[0][1])))
                     n = _send(g, core, T, topo, r, dests)
-                    g.wait_ge(S.sent, n)
+                    g.wait_ge(S.sent, n + _bits(cm))
         return
     r = rank
-    A, X, F = AluOpType, AxisListType.X, ActivationFunctionType
     te, ve, se, sy = g.tensor, g.vector, g.scalar, g.sync
     pb = [T["pb%d" % b] for b in range(8)]
     own = T.ws[:, r * D:(r + 1) * D]
     plan = _plan(T, topo, r)
-
-    eta, inc = {r: -1}, {}
-    for s in range(N):
-        if s == r:
-            continue
-        for j, (c, dests) in enumerate(_plan(T, topo, s)):
-            if r in dests:
-                eta[s] = dests.index(r) + (HOP if j else 0)
-                m = topo.mask(c, T.cores[dests[0]])
-                for d in dests:
-                    m &= topo.mask(c, T.cores[d])
-                inc[s] = _bits(m)
-    order = sorted(range(N), key=lambda s: (eta[s], (r - s) % N))
+    order, inc = _order(T, topo, r)
 
     sy.dma_start(T.wd[:, :], T.w[:, :]).then_inc(S.wdl, 16)
     se.dma_start(T.x2[:, 0:TOK], T.x[:, :]).then_inc(S.xa, 16)
@@ -107,13 +150,16 @@ def rank_program(g, core, T, topo):
     sy.dma_start(own, T.w[:, :]).then_inc(S.w, 16)
 
     ve.memset(T.ident[:, :], 1.0).then_inc(S.m1, 1)
-    ve.memset(T.ones[:, :], 1.0).then_inc(S.m2, 1)
-    ve.memset(T.negb[:, :], -BIG).then_inc(S.nb, 1)
+    ve.memset(T.ones[:, :], 0.0).then_inc(S.m2, 1)
+    ve.memset(T.nga[:, :], BA).then_inc(S.nb, 1)
+    ve.memset(T.ngb[:, :], BB).then_inc(S.nb, 1)
+    se.wait_ge(S.m2, 1)
+    se.activation(T.ones[:, :], T.ones[:, :], F.Exp).then_inc(S.on, 1)
     g.wait_ge(S.m1, 1)
     g.affine_select(T.ident[:, :], T.ident[:, :], [[-1, 128]], A.is_equal, 0.0, 0, 1).then_inc(S.id, 1)
 
     hs = [c for c, dests in plan[1:] if dests]
-    hm = topo.mask(core, hs[0]) & topo.mask(core, T.cores[plan[0][1][0]])
+    hm = topo.mask(core, hs[0]) & _smask(T, topo, core, plan[0][1])
     ids = []
     for c in hs:
         rid, pid = topo.addr(c, core)
@@ -125,19 +171,18 @@ def rank_program(g, core, T, topo):
     sent += _send(g, core, T, topo, r, plan[0][1])
 
     ve.wait_ge(S.id, 1)
-    ve.wait_ge(S.m2, 1)
     ve.tensor_scalar(T.bigi[0:N, 0:N], T.ident[0:N, 0:N], BIG, None, A.mult).then_inc(S.big, 1)
-    for e in range(N):
-        ve.tensor_scalar(T.sel[0:N, e * 128:(e + 1) * 128], T.ones[0:N, :], T.ident[0:N, e:e + 1], None, A.mult).then_inc(S.sel, 1)
+    for s in range(NL):
+        e = order[s]
+        ve.tensor_scalar(T.sel[0:N, s * 128:(s + 1) * 128], T.ident[0:N, :], 0.0, T.ident[0:N, e:e + 1], A.mult, A.add).then_inc(S.sel, 1)
 
     sc = [pb[0], pb[7]]
     te.wait_ge(S.rm, 16)
     te.wait_ge(S.big, 1)
-    te.wait_ge(S.m2, 1)
-    te.wait_ge(S.nb, 1)
+    te.wait_ge(S.nb, 2)
     for c in range(2):
         te.matmul(sc[c][:, 0:N], T.rm_sb[0:N, c * 128:(c + 1) * 128], T.bigi[0:N, 0:N], True, False)
-        te.matmul(sc[c][:, 0:N], T.ones[0:1, 0:128], T.negb[0:1, 0:N], False, False)
+        te.matmul(sc[c][:, 0:N], T.nga[0:1, 0:128], T.ngb[0:1, 0:N], False, False)
     te.wait_ge(S.xa, 16)
     te.wait_ge(S.rt, 16)
     for c in range(2):
@@ -164,12 +209,19 @@ def rank_program(g, core, T, topo):
         ve.tensor_scalar(T.dg[:, c * 128:(c + 1) * 128], T.ident[:, :], T.rinv[:, c:c + 1], None, A.mult).then_inc(S.dg, 1)
 
     te.wait_ge(S.gs, 1)
-    te.wait_ge(S.sel, N)
+    te.wait_ge(S.sel, NL)
     for b in range(6):
         for h in range(2):
-            e = order[2 * b + h]
-            te.matmul(pb[1 + b][:, h * TOK:(h + 1) * TOK], T.sel[0:N, e * 128:(e + 1) * 128], T.g_sb[0:N, :], True, True).then_inc(S["gb%d" % b], 1)
+            s = 2 * b + h
+            if s < NL:
+                lhs = T.sel[0:N, s * 128:(s + 1) * 128]
+            else:
+                j = s - NL
+                te.wait_ge(S["ch%d" % j], _bits(topo.mask(plan[1 + j][0], core) & _smask(T, topo, plan[1 + j][0], plan[1 + j][1])))
+                lhs = T.selh[0:N, j * 128:(j + 1) * 128]
+            te.matmul(pb[1 + b][:, h * TOK:(h + 1) * TOK], lhs, T.g_sb[0:N, :], True, True).then_inc(S["gb%d" % b], 1)
     te.wait_ge(S.dg, 2)
+    te.wait_ge(S.on, 1)
     for c in range(2):
         te.matmul(pb[0][:, c * 128:(c + 1) * 128], T.ones[:, :], T.dg[:, c * 128:(c + 1) * 128], True, True).then_inc(S.rs, 1)
     ve.wait_ge(S.xa, 16)

from concourse.bass import DstId, RemoteDMATransfer
from concourse.mybir import AluOpType, AxisListType, ActivationFunctionType

N, TOK, D = 12, 256, 128
NH = 3
Q_RANK = 3
Q_NEAR = 2
Q_FAR = 3
LAG = 1.2
NL = N - NH
BIG = 2.0 ** 93
BA, BB = -(2.0 ** 47), 2.0 ** 46

SCRATCH = {
    "ws": ("sbuf", [128, N * D], "bfloat16"),
    "wd": ("dram", [128, D], "bfloat16"),
    "x2": ("sbuf", [128, 2 * TOK], "bfloat16"),
    "rt_sb": ("sbuf", [128, N], "bfloat16"),
    "rm_sb": ("sbuf", [128, TOK], "bfloat16"),
    "ident": ("sbuf", [128, 128], "bfloat16"),
    "ones": ("sbuf", [128, 128], "bfloat16"),
    "nga": ("sbuf", [128, 128], "bfloat16"),
    "ngb": ("sbuf", [128, 16], "bfloat16"),
    "bigi": ("sbuf", [128, 16], "bfloat16"),
    "sel": ("sbuf", [128, NL * 128], "bfloat16"),
    "selh": ("sbuf", [128, NH * 128], "bfloat16"),
    "hs": ("sbuf", [128, 128], "bfloat16"),
    "negm": ("sbuf", [128, 2], "float32"),
    "et": ("sbuf", [128, 2 * N], "bfloat16"),
    "sums": ("sbuf", [128, 2], "float32"),
    "rinv": ("sbuf", [128, 2], "float32"),
    "dg": ("sbuf", [128, TOK], "bfloat16"),
    "rsp": ("sbuf", [128, TOK], "float32"),
    "g_sb": ("sbuf", [128, TOK], "bfloat16"),
    "xg": ("sbuf", [128, N * TOK], "bfloat16"),
    "y_sb": ("sbuf", [128, TOK], "bfloat16"),
}
for _b in range(8):
    SCRATCH["pb%d" % _b] = ("psum", [128, 512], "float32")

SEMAPHORES = (["w", "wdl", "rt", "xa", "xb", "rm", "m1", "m2", "on", "nb", "id", "big", "sent", "hand", "st0", "st1", "sel", "nm0",
               "nm1", "ex", "ri", "dg", "rs", "rc", "g", "gs", "y", "yc", "out"]
              + ["arr%d" % e for e in range(N)] + ["gb%d" % b for b in range(6)] + ["xg%d" % b for b in range(6)]
              + ["ch%d" % j for j in range(NH)])


def _bits(m):
    return bin(m).count("1")


def _deal(ov, pl, quotas):
    ov, pl = list(ov), list(pl)
    out = [[] for _ in quotas]
    for pos in range(max(quotas)):
        for m, q in enumerate(quotas):
            if len(out[m]) < q:
                first, second = (ov, pl) if pos % 2 == 0 else (pl, ov)
                src = first if first else second
                out[m].append(src.pop(0))
    return out


def _plan(T, topo, r):
    R = T.cores[r]
    dests = [(r + k) % N for k in range(1, N)]
    world = topo.CORES_PER_HOST * (1 + max(topo.host(q) for q in T.cores))
    here = [c for c in range(world) if c != R and topo.host(c) == topo.host(R) and topo.chip(c) == topo.chip(R)
            and all(topo.may_write(c, T.cores[d]) for d in dests)]
    here.sort(key=lambda c: (topo.die(c) == topo.die(R), c))
    here = here[:NH]
    far = [c for c in here if topo.die(c) != topo.die(R)]
    near = [c for c in here if topo.die(c) == topo.die(R)]
    mate = [d for d in dests if topo.mates(R, T.cores[d])]
    plane = [d for d in dests if topo.same_plane(R, T.cores[d])]
    cross = [d for d in dests if d not in mate and d not in plane]
    over = cross + mate
    qn = [Q_RANK] + [Q_NEAR] * len(near)
    qf = [Q_FAR] * len(far)
    no = len(over) // 2
    npl = sum(qn) - no
    ln = _deal(over[:no], plane[:npl], qn)
    lf = _deal(over[no:], plane[npl:], qf)
    return [(R, ln[0])] + list(zip(far, lf)) + list(zip(near, ln[1:]))


def _smask(T, topo, c, dests):
    m = topo.mask(c, T.cores[dests[0]])
    for d in dests:
        m &= topo.mask(c, T.cores[d])
    return m


def _order(T, topo, r):
    eta, inc = {r: -1.0}, {}
    for s in range(N):
        if s == r:
            continue
        for j, (c, dests) in enumerate(_plan(T, topo, s)):
            if r in dests:
                eta[s] = dests.index(r) + ((LAG + 0.1 * j) if j else 0.0)
                inc[s] = _bits(_smask(T, topo, c, dests))
    return sorted(range(N), key=lambda s: (eta[s], (r - s) % N)), inc


def _send(g, core, T, topo, r, dests):
    mask = _smask(T, topo, core, dests)
    ids = []
    for d in dests:
        rid, pid = topo.addr(T.cores[d], core)
        ids.append(DstId(rid=rid, pnc=pid))
    blk = T.ws[:, r * D:(r + 1) * D]
    g.remote_dma_fused([RemoteDMATransfer(dst_ids=ids, dma_engine_mask=mask, remote_sem=T.sem["arr%d" % r],
                                          srcs=[T.wd[:, :]], dsts=[blk for _ in dests], alu_op=0)], local_sem=T.sem.sent)
    return _bits(mask)


def rank_program(g, core, T, topo):
    S = T.sem
    A, X, F = AluOpType, AxisListType.X, ActivationFunctionType
    rank = T.rank_of(core)
    if rank is None:
        for r in range(N):
            for j, (c, dests) in enumerate(_plan(T, topo, r)[1:]):
                if c == core and dests:
                    R = T.cores[r]
                    e = _order(T, topo, r)[0][NL + j]
                    g.vector.memset(T.hs[:, :], 1.0).then_inc(S.m1, 1)
                    g.wait_ge(S.m1, 1)
                    g.affine_select(T.hs[:, :], T.hs[:, :], [[0, 128]], A.is_equal, 0.0, -e, 1).then_inc(S.id, 1)
                    g.wait_ge(S.id, 1)
                    cm = topo.mask(core, R) & _smask(T, topo, core, dests)
                    rid, pid = topo.addr(R, core)
                    g.remote_dma(T.selh[:, j * 128:(j + 1) * 128], T.hs[:, :], S["ch%d" % j], S.sent, pid, rid, cm)
                    g.wait_ge(S.hand, _bits(topo.mask(R, core) & _smask(T, topo, R, _plan(T, topo, r)[0][1])))
                    n = _send(g, core, T, topo, r, dests)
                    g.wait_ge(S.sent, n + _bits(cm))
        return
    r = rank
    te, ve, se, sy = g.tensor, g.vector, g.scalar, g.sync
    pb = [T["pb%d" % b] for b in range(8)]
    own = T.ws[:, r * D:(r + 1) * D]
    plan = _plan(T, topo, r)
    order, inc = _order(T, topo, r)

    sy.dma_start(T.wd[:, :], T.w[:, :]).then_inc(S.wdl, 16)
    se.dma_start(T.x2[:, 0:TOK], T.x[:, :]).then_inc(S.xa, 16)
    sy.dma_start(T.rm_sb[0:N, :], T.rm[:, :]).then_inc(S.rm, 16)
    se.dma_start(T.rt_sb[:, :], T.rt[:, :]).then_inc(S.rt, 16)
    sy.dma_start(T.x2[:, TOK:2 * TOK], T.x[:, :]).then_inc(S.xb, 16)
    sy.dma_start(own, T.w[:, :]).then_inc(S.w, 16)

    ve.memset(T.ident[:, :], 1.0).then_inc(S.m1, 1)
    ve.memset(T.ones[:, :], 0.0).then_inc(S.m2, 1)
    ve.memset(T.nga[:, :], BA).then_inc(S.nb, 1)
    ve.memset(T.ngb[:, :], BB).then_inc(S.nb, 1)
    se.wait_ge(S.m2, 1)
    se.activation(T.ones[:, :], T.ones[:, :], F.Exp).then_inc(S.on, 1)
    g.wait_ge(S.m1, 1)
    g.affine_select(T.ident[:, :], T.ident[:, :], [[-1, 128]], A.is_equal, 0.0, 0, 1).then_inc(S.id, 1)

    hs = [c for c, dests in plan[1:] if dests]
    hm = topo.mask(core, hs[0]) & _smask(T, topo, core, plan[0][1])
    ids = []
    for c in hs:
        rid, pid = topo.addr(c, core)
        ids.append(DstId(rid=rid, pnc=pid))
    g.wait_ge(S.wdl, 16)
    g.remote_dma_fused([RemoteDMATransfer(dst_ids=ids, dma_engine_mask=hm, remote_sem=S.hand, srcs=[T.wd[:, :]],
                                          dsts=[T.wd[:, :] for _ in hs], alu_op=0)], local_sem=S.sent)
    sent = _bits(hm)
    sent += _send(g, core, T, topo, r, plan[0][1])

    ve.wait_ge(S.id, 1)
    ve.tensor_scalar(T.bigi[0:N, 0:N], T.ident[0:N, 0:N], BIG, None, A.mult).then_inc(S.big, 1)
    for s in range(NL):
        e = order[s]
        ve.tensor_scalar(T.sel[0:N, s * 128:(s + 1) * 128], T.ident[0:N, :], 0.0, T.ident[0:N, e:e + 1], A.mult, A.add).then_inc(S.sel, 1)

    sc = [pb[0], pb[7]]
    te.wait_ge(S.rm, 16)
    te.wait_ge(S.big, 1)
    te.wait_ge(S.nb, 2)
    for c in range(2):
        te.matmul(sc[c][:, 0:N], T.rm_sb[0:N, c * 128:(c + 1) * 128], T.bigi[0:N, 0:N], True, False)
        te.matmul(sc[c][:, 0:N], T.nga[0:1, 0:128], T.ngb[0:1, 0:N], False, False)
    te.wait_ge(S.xa, 16)
    te.wait_ge(S.rt, 16)
    for c in range(2):
        te.matmul(sc[c][:, 0:N], T.x2[:, c * 128:(c + 1) * 128], T.rt_sb[:, :], False, True).then_inc(S["st%d" % c], 1)

    for c in range(2):
        ve.wait_ge(S["st%d" % c], 1)
        ve.tensor_reduce(T.negm[:, c:c + 1], sc[c][:, 0:N], X, A.max, negate=True).then_inc(S["nm%d" % c], 1)
    for c in range(2):
        se.wait_ge(S["nm%d" % c], 1)
        se.activation(T.et[:, c * N:(c + 1) * N], sc[c][:, 0:N], F.Exp, bias=T.negm[:, c:c + 1], scale=1.0,
                      accum_out=T.sums[:, c:c + 1]).then_inc(S.ex, 1)

    te.wait_ge(S.ex, 2)
    te.wait_ge(S.id, 1)
    for c in range(2):
        te.matmul(pb[0][0:N, 256 + c * 128:256 + (c + 1) * 128], T.et[:, c * N:(c + 1) * N], T.ident[:, :], True, True).then_inc(S.g, 1)
    ve.wait_ge(S.g, 2)
    ve.tensor_copy(T.g_sb[0:N, :], pb[0][0:N, 256:512]).then_inc(S.gs, 1)
    ve.wait_ge(S.ex, 2)
    ve.reciprocal(T.rinv[:, :], T.sums[:, :]).then_inc(S.ri, 1)
    ve.wait_ge(S.ri, 1)
    for c in range(2):
        ve.tensor_scalar(T.dg[:, c * 128:(c + 1) * 128], T.ident[:, :], T.rinv[:, c:c + 1], None, A.mult).then_inc(S.dg, 1)

    te.wait_ge(S.gs, 1)
    te.wait_ge(S.sel, NL)
    for b in range(6):
        for h in range(2):
            s = 2 * b + h
            if s < NL:
                lhs = T.sel[0:N, s * 128:(s + 1) * 128]
            else:
                j = s - NL
                te.wait_ge(S["ch%d" % j], _bits(topo.mask(plan[1 + j][0], core) & _smask(T, topo, plan[1 + j][0], plan[1 + j][1])))
                lhs = T.selh[0:N, j * 128:(j + 1) * 128]
            te.matmul(pb[1 + b][:, h * TOK:(h + 1) * TOK], lhs, T.g_sb[0:N, :], True, True).then_inc(S["gb%d" % b], 1)
    te.wait_ge(S.dg, 2)
    te.wait_ge(S.on, 1)
    for c in range(2):
        te.matmul(pb[0][:, c * 128:(c + 1) * 128], T.ones[:, :], T.dg[:, c * 128:(c + 1) * 128], True, True).then_inc(S.rs, 1)
    ve.wait_ge(S.xa, 16)
    ve.wait_ge(S.xb, 16)
    for b in range(6):
        ve.wait_ge(S["gb%d" % b], 2)
        ve.tensor_tensor(T.xg[:, b * 512:(b + 1) * 512], pb[1 + b][:, :], T.x2[:, :], A.mult).then_inc(S["xg%d" % b], 1)
    ve.wait_ge(S.rs, 2)
    ve.tensor_copy(T.rsp[:, :], pb[0][:, 0:TOK]).then_inc(S.rc, 1)

    for s, e in enumerate(order):
        if s % 2 == 0:
            te.wait_ge(S["xg%d" % (s // 2)], 1)
        if e == r:
            te.wait_ge(S.w, 16)
        else:
            te.wait_ge(S["arr%d" % e], inc[e])
        mm = te.matmul(pb[7][:, 0:TOK], T.ws[:, e * D:(e + 1) * D], T.xg[:, s * TOK:(s + 1) * TOK], s == 0, s == N - 1)
    mm.then_inc(S.y, 1)
    ve.wait_ge(S.rc, 1)
    ve.wait_ge(S.y, 1)
    ve.tensor_tensor(T.y_sb[:, :], pb[7][:, 0:TOK], T.rsp[:, :], A.mult).then_inc(S.yc, 1)
    sy.wait_ge(S.yc, 1)
    sy.dma_start(T.y[:, :], T.y_sb[:, :]).then_inc(S.out, 16)
    sy.wait_ge(S.out, 16)
    g.wait_ge(S.sent, sent)
